import numpy as np
import ml_dtypes


def mxq(x, axis, fmt="e4m3"):
    dtype, down = {"e4m3": (ml_dtypes.float8_e4m3fn, 7), "e5m2": (ml_dtypes.float8_e5m2, 14)}[fmt]
    v = np.moveaxis(np.asarray(x, np.float32).astype(ml_dtypes.bfloat16).astype(np.float64), axis, -1)
    blocks = v.reshape(v.shape[:-1] + (-1, 32))
    amax = np.abs(blocks).max(-1, keepdims=True)
    byte = np.maximum(np.where(amax > 0, np.frexp(amax)[1] - 1 + 127, 0) - down, 1)
    scale = np.exp2(byte - 127.0)
    codes = (blocks / scale).astype(np.float32).astype(dtype).astype(np.float64)
    return np.moveaxis((codes * scale).reshape(v.shape), -1, axis)


WIDE = False


def mx_kscale(k):
    if not WIDE:
        return np.ones(k)
    levels = np.array([10, -10, 5, -5, 0])
    if k % 512:
        return np.exp2(np.random.permutation(np.resize(levels, k // 32))).repeat(32)
    a = np.empty((k // 512, 16))
    for p in range(k // 512):
        a[p, :8] = np.random.permutation(np.resize(levels, 8))
        for g in range(8):
            far = levels[np.abs(levels - a[p, g]) >= 10]
            a[p, g + 8] = far[np.random.randint(len(far))]
    return np.exp2(a.ravel()).repeat(32)


def f64(x):
    return np.asarray(x).astype(np.float64)


def striped(idx):
    return np.tile(idx.reshape(-1, 16).T, (8, 1)).astype(np.uint16)


def unstriped(offs):
    return offs[:16].T.reshape(-1).astype(np.int64)


E2M1 = np.array([0.0, 0.5, 1.0, 1.5, 2.0, 3.0, 4.0, 6.0, -0.0, -0.5, -1.0, -1.5, -2.0, -3.0, -4.0, -6.0])


def pack_weight(w, fmt):
    k, n = w.shape
    w = f64(np.asarray(w, np.float32).astype(ml_dtypes.bfloat16)).reshape(k // 32, 32, n)
    amax = np.abs(w).max(1)
    if fmt == "e4m3":
        byte = np.frexp(amax)[1] - 1 + 127 - 7
    else:
        mant, ex = np.frexp(amax / 6.0)
        byte = np.where(mant > 0.5, ex, ex - 1) + 127
    byte = np.clip(np.where(amax > 0, byte, 1), 1, 254)
    scaled = (w * np.exp2(127.0 - byte)[:, None, :]).reshape(k, n).astype(np.float32)
    by_word = np.ascontiguousarray(scaled.reshape(k // 512, 128, 4, n).transpose(0, 1, 3, 2))
    if fmt == "e4m3":
        words = by_word.astype(ml_dtypes.float8_e4m3fn).view(np.uint8)
    else:
        c = by_word.astype(ml_dtypes.float4_e2m1fn).view(np.uint8) & 0xF
        words = (c[..., 0::2] | (c[..., 1::2] << 4)).reshape(k // 512, 128, 2 * n)
    return np.ascontiguousarray(words), np.ascontiguousarray(byte.astype(np.uint8).reshape(k // 512, 16, n))


def unpack_weight(words, scales, fmt):
    g, _, n = scales.shape
    words = np.ascontiguousarray(words).reshape(g, 128, n, -1)
    if fmt == "e4m3":
        vals = words.view(ml_dtypes.float8_e4m3fn).astype(np.float64)
    else:
        nib = np.empty((g, 128, n, 4), np.uint8)
        nib[..., 0::2] = words & 0xF
        nib[..., 1::2] = words >> 4
        vals = E2M1[nib]
    vals = vals * np.repeat(np.exp2(scales.astype(np.float64) - 127.0), 8, axis=1)[..., None]
    return vals.transpose(0, 1, 3, 2).reshape(g * 512, n)


def gelu(v):
    return 0.5 * v * (1.0 + np.tanh(np.sqrt(2.0 / np.pi) * (v + 0.044715 * v**3)))


K, K2, H, N, T, TB, S, P = 512, 1024, 1024, 256, 4096, 2048, 1024, 512

def setup_inputs():
    n = np.random.standard_normal
    s = mx_kscale(K)[:, None]
    s2 = mx_kscale(K2)[:, None]
    u = mx_kscale(H)[:, None]
    d = {}
    d["tab_words"], d["tab_scales"] = pack_weight(n((K, T)) * s, "e4m3")
    d["tab2_words"], d["tab2_scales"] = pack_weight(n((K2, TB)) * s2, "e4m3")
    d["offs"] = striped(np.random.permutation(T)[:S])
    d["offs2"] = striped(np.random.permutation(TB)[:P])
    d["pos1"] = striped(np.random.permutation(S)[:P])
    d["w1"] = (n((K, H)) / K**0.5 / s * u.T).astype(np.float32)
    d["rest"] = (0.5 * n(H) * u[:, 0]).astype(np.float32)
    d["w2_words"], d["w2_scales"] = pack_weight(0.8 * n((K2, H)) / K2**0.5 / s2, "e2m1")
    d["w3"] = (2.0 * n((K2, H)) / K2**0.5 / s2).astype(np.float32)
    d["gain"] = (0.4 * n(H) * u[:, 0]).astype(np.float32)
    d["wgs"] = np.exp(0.3 * n((128, P))).astype(np.float32)
    d["w4_words"], d["w4_scales"] = pack_weight(0.46 * n((H, N)) / H**0.5 / u, "e4m3")
    return d

def reference(tab_words, tab_scales, tab2_words, tab2_scales, offs, offs2, pos1, w1, rest, w2_words, w2_scales, w3, gain, wgs, w4_words, w4_scales):
    v = unpack_weight(tab_words, tab_scales, "e4m3")[:, unstriped(offs)]
    v2 = unpack_weight(tab2_words, tab2_scales, "e4m3")[:, unstriped(offs2)]
    a = np.maximum(mxq(f64(w1), 0, "e4m3").T @ v, f64(rest)[:, None])
    raw = unpack_weight(w2_words, w2_scales, "e2m1").T @ v2
    bounded = np.tanh(mxq(f64(w3), 0, "e4m3").T @ v2)
    b = f64(gain)[:, None] * np.square(raw - bounded)
    placed = np.zeros((H, S))
    placed[:, unstriped(pos1)] = np.tile(f64(wgs), (H // 128, 1)) * b
    z = a + placed
    zq = mxq(z, 0, "e4m3")
    out = np.sin(unpack_weight(w4_words, w4_scales, "e4m3").T @ zq)
    return out

@@ -1,0 +1,299 @@
+from contextlib import ExitStack
+
+import concourse.mybir as mybir
+from concourse.masks import make_identity
+
+K, K2, H, N, T, TB, S, PL = 512, 1024, 1024, 256, 4096, 2048, 1024, 512
+FLOPS = 2 * (K * H * S + 2 * K2 * H * PL + H * N * S)
+
+F32 = mybir.dt.float32
+BF16 = mybir.dt.bfloat16
+I32 = mybir.dt.int32
+U32 = mybir.dt.uint32
+U16 = mybir.dt.uint16
+U8 = mybir.dt.uint8
+FP8X4 = mybir.dt.float8_e4m3fn_x4
+FP4X4 = mybir.dt.float4_e2m1fn_x4
+ACT = mybir.ActivationFunctionType
+ALU = mybir.AluOpType
+
+P = 128
+PACK = 4
+PASS = P * PACK
+QUADS = 4
+BANK = 512
+PIECE = 256
+
+
+def tile_list_gloss_timing_features_kernel(
+    tc, tab_words, tab_scales, tab2_words, tab2_scales, offs, offs2, pos1, w1, rest, w2_words, w2_scales, w3, gain, wgs,
+    w4_words, w4_scales, out,
+):
+    nc = tc.nc
+    with ExitStack() as ctx:
+        lists = ctx.enter_context(tc.tile_pool(name="lists", bufs=1))
+        keep = ctx.enter_context(tc.tile_pool(name="keep", bufs=1))
+        ring = ctx.enter_context(tc.tile_pool(name="ring", bufs=1))
+        psum = ctx.enter_context(tc.psum_pool(name="psum", bufs=1))
+
+        def held(name, shape, dtype):
+            return keep.tile(shape, dtype, name=name, align_bytes=64)
+
+        def staged(tag, shape, dtype, bufs):
+            return ring.tile(shape, dtype, name=tag, tag=tag, bufs=bufs, align_bytes=64)
+
+        def bank(tag, bufs):
+            return psum.tile([P, BANK], F32, name=tag, tag=tag, bufs=bufs)
+
+        def load_scale_rows(plane, scales, queue=nc.sync):
+            for q in range(QUADS):
+                queue.dma_start(
+                    plane[32 * q : 32 * q + 4, :, :].bitcast(I32),
+                    scales[:, 4 * q : 4 * q + 4, :].rearrange("a r c -> r a c").bitcast(I32),
+                )
+
+        def load_weight_rows(w, a, b):
+            raw = staged("w_raw", [P, PACK, PASS], F32, 4)
+            nc.sync.dma_start(raw[:], w[a * PASS : (a + 1) * PASS, b * PASS : (b + 1) * PASS].rearrange("(p i) c -> p i c", i=PACK))
+            return raw
+
+        def quantize(name, grouped):
+            codes = held(name + "_codes", [P, PASS], I32)
+            plane = held(name + "_scales", [P, PASS], U8)
+            nc.vector.quantize_mx(out=codes[:].bitcast(FP8X4), scales=plane[:], in_=grouped[:])
+            return codes, plane
+
+        zero_in = held("zero_in", [P, 1], F32)
+        zero = held("zero", [P, 1], F32)
+        nc.vector.memset(zero_in[:], 0.0)
+        nc.scalar.activation(zero[:], zero_in[:], ACT.Silu)
+
+        tab2_plane = held("tab2_plane", [P, 2, TB], U8)
+        w2_plane = held("w2_plane", [P, 2, H], U8)
+        tab_plane = held("tab_plane", [P, 1, T], U8)
+        w4_plane = held("w4_plane", [P, 2, N], U8)
+        nc.vector.memset(tab2_plane[:].bitcast(I32), 0)
+        nc.vector.memset(w2_plane[:].bitcast(I32), 0)
+        pages = [[held("page%d%d" % (b, t), [P, S], F32) for t in range(PACK)] for b in range(2)]
+        for t in range(PACK):
+            nc.vector.memset(pages[0][t][:], 0.0)
+        nc.gpsimd.memset(tab_plane[:].bitcast(I32), 0)
+        load_scale_rows(tab_plane, tab_scales, nc.gpsimd)
+        ident = held("ident", [P, P], F32)
+        make_identity(nc, ident[:])
+        nc.gpsimd.memset(w4_plane[:].bitcast(I32), 0)
+        for t in range(PACK):
+            nc.gpsimd.memset(pages[1][t][:], 0.0)
+
+        offs2_sb = lists.tile([P, PL // 16], U16, name="offs2_sb")
+        pos_sb = lists.tile([P, PL // 16], U16, name="pos_sb")
+        offs_sb = lists.tile([P, S // 16], U16, name="offs_sb")
+        nc.sync.dma_start(offs2_sb[:], offs2)
+        tab2_sb = [held("tab2_sb%d" % a, [P, TB], I32) for a in range(2)]
+        nc.sync.dma_start(tab2_sb[0][:], tab2_words[0].rearrange("p t i -> p (t i)").bitcast(I32))
+        load_scale_rows(tab2_plane, tab2_scales)
+        nc.sync.dma_start(tab2_sb[1][:], tab2_words[1].rearrange("p t i -> p (t i)").bitcast(I32))
+
+        w2_sb = [held("w2_sb%d" % b, [P, 2, 2 * PASS], U8) for b in range(2)]
+
+        def load_w2(b):
+            nc.sync.dma_start(
+                w2_sb[b][:].bitcast(I32),
+                w2_words[:, :, 2 * PASS * b : 2 * PASS * (b + 1)].rearrange("a p c -> p a c").bitcast(I32),
+            )
+
+        wgs_dealt = [held("wgs_dealt%d" % h, [P, PACK, PIECE], F32) for h in range(2)]
+
+        def load_wgs(h):
+            for q in range(QUADS):
+                nc.sync.dma_start(
+                    wgs_dealt[h][32 * q : 32 * (q + 1), :, :],
+                    wgs[:, h * PIECE : (h + 1) * PIECE].rearrange("(r t) j -> r t j", t=PACK),
+                )
+
+        gain_sb = [held("gain_sb%d" % b, [P, PACK], F32) for b in range(2)]
+        rest_sb = held("rest_sb", [P, 2, PACK], F32)
+
+        def load_gain(b):
+            nc.sync.dma_start(gain_sb[b][:], gain[b * PASS : (b + 1) * PASS].rearrange("(p t) -> p t", t=PACK))
+
+        load_w2(0)
+        load_scale_rows(w2_plane, w2_scales)
+        load_gain(0)
+        w3_raw = [[None, None], [None, None]]
+        w3_raw[0][0] = load_weight_rows(w3, 0, 0)
+        w3_raw[0][1] = load_weight_rows(w3, 1, 0)
+        load_wgs(0)
+        nc.sync.dma_start(offs_sb[:], offs)
+        nc.sync.dma_start(pos_sb[:], pos1)
+        load_wgs(1)
+        w3_raw[1][0] = load_weight_rows(w3, 0, 1)
+        w3_raw[1][1] = load_weight_rows(w3, 1, 1)
+        load_w2(1)
+        tab_sb = held("tab_sb", [P, T], I32)
+        nc.sync.dma_start(tab_sb[:], tab_words[0].rearrange("p t i -> p (t i)").bitcast(I32))
+        load_gain(1)
+        w1_raw = [load_weight_rows(w1, 0, 0)]
+        nc.sync.dma_start(rest_sb[:], rest.rearrange("(b p t) -> p b t", b=2, t=PACK))
+        w1_raw.append(load_weight_rows(w1, 0, 1))
+        w4_sb = held("w4_sb", [P, 2, N], I32)
+        nc.sync.dma_start(w4_sb[:], w4_words.rearrange("a p c i -> p a (c i)").bitcast(I32))
+        load_scale_rows(w4_plane, w4_scales)
+
+        v2_codes, v2_scales = [], []
+        for a in range(2):
+            plane = held("v2_scales%d" % a, [P, PL], U8)
+            nc.vector.tensor_copy(plane[:], tab2_plane[:, a, :].indirect(offs2_sb[:]))
+            codes = held("v2_codes%d" % a, [P, PL], I32)
+            nc.vector.tensor_copy(codes[:].bitcast(U32), tab2_sb[a][:].bitcast(U32).indirect(offs2_sb[:]))
+            v2_codes.append(codes)
+            v2_scales.append(plane)
+
+        def group_w3(b, a, engine_copy):
+            grouped = staged("grouped", [P, PASS * PACK], BF16, 4)
+            engine_copy(
+                grouped[:].rearrange("p (c n i) -> p c i n", n=4, i=PACK),
+                w3_raw[b][a][:].rearrange("p i (c n) -> p c i n", n=4),
+            )
+            return grouped
+
+        def raw_product(b, jb):
+            acc = bank("mx", 6)
+            cols = slice(jb * P, (jb + 1) * P)
+            for a in range(2):
+                nc.tensor.matmul_mx(
+                    out=acc[:], lhsT=v2_codes[a][:, cols].bitcast(FP8X4), lhsT_scale=v2_scales[a][:, cols],
+                    rhs=w2_sb[b][:, a, :].bitcast(FP4X4), rhs_scale=w2_plane[:, a, b * PASS : (b + 1) * PASS],
+                    start=(a == 0), stop=(a == 1),
+                )
+            raw_t = staged("raw_t", [P, PACK, P], F32, 4)
+            nc.scalar.copy(raw_t[:], acc[:].rearrange("j (p t) -> j t p", t=PACK))
+            return raw_t
+
+        def bounded_product(w3_q, jb, neg_t=None):
+            acc = bank("mx", 6)
+            cols = slice(jb * P, (jb + 1) * P)
+            for a in range(2):
+                nc.tensor.matmul_mx(
+                    out=acc[:], lhsT=v2_codes[a][:, cols].bitcast(FP8X4), lhsT_scale=v2_scales[a][:, cols],
+                    rhs=w3_q[a][0][:].bitcast(FP8X4), rhs_scale=w3_q[a][1][:],
+                    start=(a == 0), stop=(a == 1),
+                )
+            if neg_t is None:
+                neg_t = staged("neg_t", [P, PACK, P], F32, 4)[:]
+            nc.scalar.activation(neg_t, acc[:].rearrange("j (p t) -> j t p", t=PACK), ACT.Tanh, bias=zero[:], scale=-1.0)
+            return neg_t
+
+        def weights(b, h, g=None):
+            if g is None:
+                g = held("g%d%d" % (b, h), [P, PACK, PIECE], F32)[:]
+            for t in range(PACK):
+                if b == 0 and h == 0:
+                    nc.vector.tensor_scalar(g[:, t, :], wgs_dealt[h][:, t, :], gain_sb[b][:, t : t + 1], None, ALU.mult)
+                else:
+                    nc.scalar.activation(g[:, t, :], wgs_dealt[h][:, t, :], ACT.Copy, scale=gain_sb[b][:, t : t + 1])
+            return g
+
+        def corrections(b, h, raw_ts, neg_ts, g):
+            for pair in range(2):
+                diff = bank("diff", 2)
+                for u in range(2):
+                    t = 2 * pair + u
+                    for e in range(2):
+                        dst = diff[:, u * PIECE + e * P : u * PIECE + (e + 1) * P]
+                        nc.tensor.matmul(dst, raw_ts[e][:, t, :], ident[:], start=True, stop=False, is_transpose=True)
+                        nc.tensor.matmul(dst, neg_ts[e][:, t, :], ident[:], start=False, stop=True, is_transpose=True)
+                sq = staged("sq", [P, 2, PIECE], F32, 6)
+                nc.scalar.activation(sq[:].rearrange("p u j -> p (u j)"), diff[:], ACT.Square, bias=zero[:])
+                for u in range(2):
+                    t = 2 * pair + u
+                    nc.vector.tensor_tensor(
+                        pages[b][t][:].indirect(pos_sb[:, h * (PIECE // 16) : (h + 1) * (PIECE // 16)]),
+                        sq[:, u, :], g[:, t, :], ALU.mult,
+                    )
+
+        raw0 = [raw_product(0, jb) for jb in range(4)]
+        w3_q0 = []
+        for a in range(2):
+            w3_q0.append(quantize("w3_0%d" % a, group_w3(0, a, nc.vector.tensor_copy)))
+        neg = [bounded_product(w3_q0, jb) for jb in range(2)]
+        g00 = weights(0, 0)
+        v_scales = held("v_scales", [P, S], U8)
+        nc.vector.tensor_copy(v_scales[:], tab_plane[:, 0, :].indirect(offs_sb[:]))
+        corrections(0, 0, raw0[0:2], neg, g00)
+        g01 = weights(0, 1)
+        w3_q1 = []
+        for a in range(2):
+            w3_q1.append(quantize("w3_1%d" % a, group_w3(1, a, nc.scalar.copy)))
+        neg = [
+            bounded_product(w3_q0, 2 + a, w3_raw[1][a][:, 0, :].rearrange("p (t q) -> p t q", t=PACK)) for a in range(2)
+        ]
+        corrections(0, 1, raw0[2:4], neg, g01)
+        raw1 = [raw_product(1, jb) for jb in range(4)]
+        neg1 = [bounded_product(w3_q1, jb) for jb in range(4)]
+
+        v_codes = held("v_codes", [P, S], I32)
+        nc.vector.tensor_copy(v_codes[:].bitcast(U32), tab_sb[:].bitcast(U32).indirect(offs_sb[:]))
+
+        def group_w1(b):
+            grouped = staged("grouped", [P, PASS * PACK], BF16, 4)
+            nc.scalar.copy(
+                grouped[:].rearrange("p (t m i) -> p m i t", t=PACK, i=PACK),
+                w1_raw[b][:].rearrange("p i (m t) -> p m i t", t=PACK),
+            )
+            return grouped
+
+        g10 = weights(1, 0)
+        corrections(1, 0, raw1[0:2], neg1[0:2], g10)
+        w1_q = [quantize("w1_0", group_w1(0))]
+        g11 = weights(1, 1, w1_raw[0][:, 0:2, :].rearrange("p u (v j) -> p (u v) j", v=2))
+        corrections(1, 1, raw1[2:4], neg1[2:4], g11)
+        w1_q.append(quantize("w1_1", group_w1(1)))
+
+        def combine(b, c0, width, weave):
+            cols = slice(c0, c0 + width)
+            z = staged("z", [P, PACK, width], BF16, 2) if b == 0 else staged("sq", [P, PACK, width], BF16, 6)
+            for t in range(PACK):
+                acc = bank("mx", 6)
+                rows = slice(t * P, (t + 1) * P)
+                nc.tensor.matmul_mx(
+                    out=acc[:, :width], lhsT=w1_q[b][0][:, rows].bitcast(FP8X4), lhsT_scale=w1_q[b][1][:, rows],
+                    rhs=v_codes[:, cols].bitcast(FP8X4), rhs_scale=v_scales[:, cols], start=True, stop=True,
+                )
+                nc.vector.scalar_tensor_tensor(
+                    z[:, t, :], acc[:, :width], rest_sb[:, b, t : t + 1], pages[b][t][:, cols], ALU.max, ALU.add
+                )
+            grouped = staged("grouped", [P, width * PACK], BF16, 4) if b == 0 else staged("grouped1", [P, width * PACK], BF16, 4)
+            weave(
+                grouped[:].rearrange("p (c n t) -> p c t n", n=4, t=PACK),
+                z[:].rearrange("p t (c n) -> p c t n", n=4),
+            )
+            return grouped
+
+        z_codes = [held("z_codes%d" % b, [P, S], I32) for b in range(2)]
+        z_scales = [held("z_scales%d" % b, [P, S], U8) for b in range(2)]
+
+        def quantize_z(b, c0, width, grouped):
+            cols = slice(c0, c0 + width)
+            nc.vector.quantize_mx(out=z_codes[b][:, cols].bitcast(FP8X4), scales=z_scales[b][:, cols], in_=grouped[:])
+
+        z_grouped0 = [combine(0, half * BANK, BANK, nc.scalar.copy) for half in range(2)]
+        chunks = [(0, 256), (256, 256), (512, 256), (768, 256)]
+        for half in range(2):
+            quantize_z(0, half * BANK, BANK, z_grouped0[half])
+        z_grouped1 = [combine(1, c0, width, nc.vector.tensor_copy if c0 == 768 else nc.scalar.copy) for c0, width in chunks]
+        for (c0, width), grouped in zip(chunks, z_grouped1):
+            quantize_z(1, c0, width, grouped)
+            cols = slice(c0, c0 + width)
+            for nt in range(2):
+                acc = bank("mx", 6)
+                rows = slice(nt * P, (nt + 1) * P)
+                for b in range(2):
+                    nc.tensor.matmul_mx(
+                        out=acc[:, :width], lhsT=w4_sb[:, b, rows].bitcast(FP8X4), lhsT_scale=w4_plane[:, b, rows],
+                        rhs=z_codes[b][:, cols].bitcast(FP8X4), rhs_scale=z_scales[b][:, cols],
+                        start=(b == 0), stop=(b == 1),
+                    )
+                res = staged(("raw_t", "neg_t")[nt], [P, width], F32, 4)
+                nc.scalar.activation(res[:], acc[:, :width], ACT.Sin, bias=zero[:])
+                nc.sync.dma_start(out[rows, cols], res[:])

@@ -21,6 +21,7 @@ P = 128
 PACK = 4
 PASS = P * PACK
 QUADS = 4
+QUAD_ORDER = (0, 2, 1, 3)
 BANK = 512
 PIECE = 256
 
@@ -42,12 +43,12 @@ def tile_list_gloss_timing_features_kernel(
         def staged(tag, shape, dtype, bufs):
             return ring.tile(shape, dtype, name=tag, tag=tag, bufs=bufs, align_bytes=64)
 
-        def bank(tag, bufs):
-            return psum.tile([P, BANK], F32, name=tag, tag=tag, bufs=bufs)
+        def bank(n):
+            return psum.tile([P, BANK], F32, name="bank%d" % n, tag="bank%d" % n)
 
-        def load_scale_rows(plane, scales, queue=nc.sync):
-            for q in range(QUADS):
-                queue.dma_start(
+        def load_scale_rows(plane, scales):
+            for q in QUAD_ORDER:
+                nc.sync.dma_start(
                     plane[32 * q : 32 * q + 4, :, :].bitcast(I32),
                     scales[:, 4 * q : 4 * q + 4, :].rearrange("a r c -> r a c").bitcast(I32),
                 )
@@ -63,198 +64,201 @@ def tile_list_gloss_timing_features_kernel(
             nc.vector.quantize_mx(out=codes[:].bitcast(FP8X4), scales=plane[:], in_=grouped[:])
             return codes, plane
 
-        zero_in = held("zero_in", [P, 1], F32)
-        zero = held("zero", [P, 1], F32)
-        nc.vector.memset(zero_in[:], 0.0)
-        nc.scalar.activation(zero[:], zero_in[:], ACT.Silu)
-
         tab2_plane = held("tab2_plane", [P, 2, TB], U8)
-        w2_plane = held("w2_plane", [P, 2, H], U8)
+        w2_plane = [held("w2_plane%d" % b, [P, 2, PASS], U8) for b in range(2)]
         tab_plane = held("tab_plane", [P, 1, T], U8)
         w4_plane = held("w4_plane", [P, 2, N], U8)
+        zero_in = held("zero_in", [P, 1], F32)
+        zero = held("zero", [P, 1], F32)
         nc.vector.memset(tab2_plane[:].bitcast(I32), 0)
-        nc.vector.memset(w2_plane[:].bitcast(I32), 0)
-        pages = [[held("page%d%d" % (b, t), [P, S], F32) for t in range(PACK)] for b in range(2)]
-        for t in range(PACK):
-            nc.vector.memset(pages[0][t][:], 0.0)
-        nc.gpsimd.memset(tab_plane[:].bitcast(I32), 0)
-        load_scale_rows(tab_plane, tab_scales, nc.gpsimd)
+        nc.vector.memset(w2_plane[0][:].bitcast(I32), 0)
+        nc.vector.memset(zero_in[:], 0.0)
+        nc.scalar.activation(zero[:], zero_in[:], ACT.Silu)
+        nc.vector.memset(tab_plane[:].bitcast(I32), 0)
+        nc.vector.memset(w2_plane[1][:].bitcast(I32), 0)
         ident = held("ident", [P, P], F32)
         make_identity(nc, ident[:])
         nc.gpsimd.memset(w4_plane[:].bitcast(I32), 0)
-        for t in range(PACK):
-            nc.gpsimd.memset(pages[1][t][:], 0.0)
+        pages = [[held("page%d%d" % (b, t), [P, S], F32) for t in range(PACK)] for b in range(2)]
+        for b in range(2):
+            for t in range(PACK):
+                nc.gpsimd.memset(pages[b][t][:], 0.0)
 
         offs2_sb = lists.tile([P, PL // 16], U16, name="offs2_sb")
         pos_sb = lists.tile([P, PL // 16], U16, name="pos_sb")
         offs_sb = lists.tile([P, S // 16], U16, name="offs_sb")
-        nc.sync.dma_start(offs2_sb[:], offs2)
         tab2_sb = [held("tab2_sb%d" % a, [P, TB], I32) for a in range(2)]
-        nc.sync.dma_start(tab2_sb[0][:], tab2_words[0].rearrange("p t i -> p (t i)").bitcast(I32))
-        load_scale_rows(tab2_plane, tab2_scales)
-        nc.sync.dma_start(tab2_sb[1][:], tab2_words[1].rearrange("p t i -> p (t i)").bitcast(I32))
-
         w2_sb = [held("w2_sb%d" % b, [P, 2, 2 * PASS], U8) for b in range(2)]
+        wgs_sb = held("wgs_sb", [P, PL], F32)
+        gain_sb = held("gain_sb", [P, 2, PACK], F32)
+        rest_sb = held("rest_sb", [P, 2, PACK], F32)
+        tab_sb = held("tab_sb", [P, T], I32)
+        w4_sb = held("w4_sb", [P, 2, N], I32)
 
-        def load_w2(b):
+        def load_w2_words(b):
             nc.sync.dma_start(
                 w2_sb[b][:].bitcast(I32),
                 w2_words[:, :, 2 * PASS * b : 2 * PASS * (b + 1)].rearrange("a p c -> p a c").bitcast(I32),
             )
 
-        wgs_dealt = [held("wgs_dealt%d" % h, [P, PACK, PIECE], F32) for h in range(2)]
+        def load_w2_scales(b):
+            cols = slice(b * PASS, (b + 1) * PASS)
+            load_scale_rows(w2_plane[b], w2_scales[:, :, cols])
 
-        def load_wgs(h):
-            for q in range(QUADS):
-                nc.sync.dma_start(
-                    wgs_dealt[h][32 * q : 32 * (q + 1), :, :],
-                    wgs[:, h * PIECE : (h + 1) * PIECE].rearrange("(r t) j -> r t j", t=PACK),
-                )
-
-        gain_sb = [held("gain_sb%d" % b, [P, PACK], F32) for b in range(2)]
-        rest_sb = held("rest_sb", [P, 2, PACK], F32)
-
-        def load_gain(b):
-            nc.sync.dma_start(gain_sb[b][:], gain[b * PASS : (b + 1) * PASS].rearrange("(p t) -> p t", t=PACK))
-
-        load_w2(0)
-        load_scale_rows(w2_plane, w2_scales)
-        load_gain(0)
+        nc.sync.dma_start(offs2_sb[:], offs2)
+        nc.sync.dma_start(wgs_sb[:], wgs)
+        load_scale_rows(tab2_plane, tab2_scales)
+        nc.sync.dma_start(tab2_sb[0][:], tab2_words[0].rearrange("p t i -> p (t i)").bitcast(I32))
+        nc.sync.dma_start(gain_sb[:], gain.rearrange("(b p t) -> p b t", b=2, t=PACK))
+        nc.sync.dma_start(tab2_sb[1][:], tab2_words[1].rearrange("p t i -> p (t i)").bitcast(I32))
         w3_raw = [[None, None], [None, None]]
+        load_w2_scales(0)
+        load_w2_words(0)
         w3_raw[0][0] = load_weight_rows(w3, 0, 0)
         w3_raw[0][1] = load_weight_rows(w3, 1, 0)
-        load_wgs(0)
         nc.sync.dma_start(offs_sb[:], offs)
+        load_scale_rows(tab_plane, tab_scales)
         nc.sync.dma_start(pos_sb[:], pos1)
-        load_wgs(1)
+        load_w2_scales(1)
         w3_raw[1][0] = load_weight_rows(w3, 0, 1)
         w3_raw[1][1] = load_weight_rows(w3, 1, 1)
-        load_w2(1)
-        tab_sb = held("tab_sb", [P, T], I32)
+        load_w2_words(1)
         nc.sync.dma_start(tab_sb[:], tab_words[0].rearrange("p t i -> p (t i)").bitcast(I32))
-        load_gain(1)
         w1_raw = [load_weight_rows(w1, 0, 0)]
         nc.sync.dma_start(rest_sb[:], rest.rearrange("(b p t) -> p b t", b=2, t=PACK))
         w1_raw.append(load_weight_rows(w1, 0, 1))
-        w4_sb = held("w4_sb", [P, 2, N], I32)
         nc.sync.dma_start(w4_sb[:], w4_words.rearrange("a p c i -> p a (c i)").bitcast(I32))
         load_scale_rows(w4_plane, w4_scales)
 
-        v2_codes, v2_scales = [], []
+        v2_scales = [held("v2_scales%d" % a, [P, PL], U8) for a in range(2)]
         for a in range(2):
-            plane = held("v2_scales%d" % a, [P, PL], U8)
-            nc.vector.tensor_copy(plane[:], tab2_plane[:, a, :].indirect(offs2_sb[:]))
+            nc.vector.tensor_copy(v2_scales[a][:], tab2_plane[:, a, :].indirect(offs2_sb[:]))
+
+        wgs_t = bank(0)
+        for jb in range(4):
+            nc.tensor.transpose(wgs_t[:, jb * P : (jb + 1) * P], wgs_sb[:, jb * P : (jb + 1) * P], ident[:])
+        spread = []
+        for jb in range(4):
+            tile = staged("neg_t", [P, PACK, QUADS, 32], F32, 4)
+            nc.vector.tensor_copy(
+                tile[:],
+                wgs_t[:, jb * P : (jb + 1) * P].rearrange("j (q t) -> j t q", t=PACK).unsqueeze(2).to_broadcast([P, PACK, QUADS, 32]),
+            )
+            spread.append(tile)
+        weight = [held("weight%d" % b, [P, PACK, PL], F32) for b in range(2)]
+        for t in range(PACK):
+            dealt = bank(1 + t)
+            for jb in range(4):
+                nc.tensor.transpose(dealt[:, jb * P : (jb + 1) * P], spread[jb][:, t, :, :].rearrange("j u q -> j (u q)"), ident[:])
+            for b in range(2):
+                nc.scalar.activation(weight[b][:, t, :], dealt[:], ACT.Copy, scale=gain_sb[:, b, t : t + 1])
+
+        v2_codes = []
+        for a in range(2):
             codes = held("v2_codes%d" % a, [P, PL], I32)
             nc.vector.tensor_copy(codes[:].bitcast(U32), tab2_sb[a][:].bitcast(U32).indirect(offs2_sb[:]))
             v2_codes.append(codes)
-            v2_scales.append(plane)
 
-        def group_w3(b, a, engine_copy):
+        def deal(raw, engine_copy):
             grouped = staged("grouped", [P, PASS * PACK], BF16, 4)
             engine_copy(
-                grouped[:].rearrange("p (c n i) -> p c i n", n=4, i=PACK),
-                w3_raw[b][a][:].rearrange("p i (c n) -> p c i n", n=4),
+                grouped[:].rearrange("p (t m i) -> p m i t", t=PACK, i=PACK),
+                raw[:].rearrange("p i (m t) -> p m i t", t=PACK),
             )
             return grouped
 
-        def raw_product(b, jb):
-            acc = bank("mx", 6)
+        def deal_pair(raw, u, engine_copy):
+            grouped = staged("grouped", [P, 2 * P * PACK], BF16, 4)
+            engine_copy(
+                grouped[:].rearrange("p (e m i) -> p m i e", e=2, i=PACK),
+                raw[:].rearrange("p i (m u e) -> p u m i e", u=2, e=2)[:, u],
+            )
+            return grouped
+
+        def raw_product(b, jb, raw_t, n):
+            acc = bank(n)
             cols = slice(jb * P, (jb + 1) * P)
             for a in range(2):
                 nc.tensor.matmul_mx(
                     out=acc[:], lhsT=v2_codes[a][:, cols].bitcast(FP8X4), lhsT_scale=v2_scales[a][:, cols],
-                    rhs=w2_sb[b][:, a, :].bitcast(FP4X4), rhs_scale=w2_plane[:, a, b * PASS : (b + 1) * PASS],
+                    rhs=w2_sb[b][:, a, :].bitcast(FP4X4), rhs_scale=w2_plane[b][:, a, :],
                     start=(a == 0), stop=(a == 1),
                 )
-            raw_t = staged("raw_t", [P, PACK, P], F32, 4)
-            nc.scalar.copy(raw_t[:], acc[:].rearrange("j (p t) -> j t p", t=PACK))
+            nc.scalar.copy(raw_t, acc[:].rearrange("j (p t) -> j t p", t=PACK))
             return raw_t
 
-        def bounded_product(w3_q, jb, neg_t=None):
-            acc = bank("mx", 6)
-            cols = slice(jb * P, (jb + 1) * P)
+        def bounded_product(w3_q, h, u, neg_t, n):
+            acc = bank(n)
+            chans = slice(u * 2 * P, (u + 1) * 2 * P)
             for a in range(2):
-                nc.tensor.matmul_mx(
-                    out=acc[:], lhsT=v2_codes[a][:, cols].bitcast(FP8X4), lhsT_scale=v2_scales[a][:, cols],
-                    rhs=w3_q[a][0][:].bitcast(FP8X4), rhs_scale=w3_q[a][1][:],
-                    start=(a == 0), stop=(a == 1),
-                )
-            if neg_t is None:
-                neg_t = staged("neg_t", [P, PACK, P], F32, 4)[:]
-            nc.scalar.activation(neg_t, acc[:].rearrange("j (p t) -> j t p", t=PACK), ACT.Tanh, bias=zero[:], scale=-1.0)
+                for e in range(2):
+                    cols = slice((2 * h + e) * P, (2 * h + e + 1) * P)
+                    nc.tensor.matmul_mx(
+                        out=acc[:, e * 2 * P : (e + 1) * 2 * P],
+                        lhsT=v2_codes[a][:, cols].bitcast(FP8X4), lhsT_scale=v2_scales[a][:, cols],
+                        rhs=w3_q[a][0][:, chans].bitcast(FP8X4), rhs_scale=w3_q[a][1][:, chans],
+                        start=(a == 0 and e == 0), stop=(a == 1 and e == 1),
+                    )
+            nc.scalar.activation(neg_t, acc[:], ACT.Tanh, bias=zero[:], scale=-1.0)
             return neg_t
 
-        def weights(b, h, g=None):
-            if g is None:
-                g = held("g%d%d" % (b, h), [P, PACK, PIECE], F32)[:]
-            for t in range(PACK):
-                if b == 0 and h == 0:
-                    nc.vector.tensor_scalar(g[:, t, :], wgs_dealt[h][:, t, :], gain_sb[b][:, t : t + 1], None, ALU.mult)
-                else:
-                    nc.scalar.activation(g[:, t, :], wgs_dealt[h][:, t, :], ACT.Copy, scale=gain_sb[b][:, t : t + 1])
-            return g
+        def fresh(tag, shape):
+            return staged(tag, shape, F32, 4)[:]
 
-        def corrections(b, h, raw_ts, neg_ts, g):
-            for pair in range(2):
-                diff = bank("diff", 2)
-                for u in range(2):
-                    t = 2 * pair + u
-                    for e in range(2):
-                        dst = diff[:, u * PIECE + e * P : u * PIECE + (e + 1) * P]
-                        nc.tensor.matmul(dst, raw_ts[e][:, t, :], ident[:], start=True, stop=False, is_transpose=True)
-                        nc.tensor.matmul(dst, neg_ts[e][:, t, :], ident[:], start=False, stop=True, is_transpose=True)
-                sq = staged("sq", [P, 2, PIECE], F32, 6)
-                nc.scalar.activation(sq[:].rearrange("p u j -> p (u j)"), diff[:], ACT.Square, bias=zero[:])
-                for u in range(2):
-                    t = 2 * pair + u
-                    nc.vector.tensor_tensor(
-                        pages[b][t][:].indirect(pos_sb[:, h * (PIECE // 16) : (h + 1) * (PIECE // 16)]),
-                        sq[:, u, :], g[:, t, :], ALU.mult,
-                    )
+        def place_pair(b, h, u, raw_ts, neg_t, n, sq):
+            diff = bank(n)
+            for v in range(2):
+                for e in range(2):
+                    dst = diff[:, v * PIECE + e * P : v * PIECE + (e + 1) * P]
+                    nc.tensor.matmul(dst, neg_t[:, (2 * e + v) * P : (2 * e + v + 1) * P], ident[:], start=True, stop=False, is_transpose=True)
+                    nc.tensor.matmul(dst, raw_ts[2 * h + e][:, 2 * u + v, :], ident[:], start=False, stop=True, is_transpose=True)
+            nc.scalar.activation(sq, diff[:], ACT.Square, bias=zero[:])
+            for v in range(2):
+                t = 2 * u + v
+                nc.vector.tensor_tensor(
+                    pages[b][t][:].indirect(pos_sb[:, h * (PIECE // 16) : (h + 1) * (PIECE // 16)]),
+                    sq[:, v * PIECE : (v + 1) * PIECE], weight[b][:, t, h * PIECE : (h + 1) * PIECE], ALU.mult,
+                )
 
-        raw0 = [raw_product(0, jb) for jb in range(4)]
-        w3_q0 = []
-        for a in range(2):
-            w3_q0.append(quantize("w3_0%d" % a, group_w3(0, a, nc.vector.tensor_copy)))
-        neg = [bounded_product(w3_q0, jb) for jb in range(2)]
-        g00 = weights(0, 0)
+        def squares():
+            return staged("sq", [P, BANK], F32, 6)[:]
+
+        raw = [raw_product(0, jb, fresh("raw_t", [P, PACK, P]), (0, 5, 6, 7)[jb]) for jb in range(4)]
+        w3_q0 = [quantize("w3_00", deal(w3_raw[0][0], nc.vector.tensor_copy))]
+        last_codes = held("w3_01_codes", [P, PASS], I32)
+        last_scales = held("w3_01_scales", [P, PASS], U8)
+        w3_q0.append((last_codes, last_scales))
+        halves = [deal_pair(w3_raw[0][1], u, (nc.vector.tensor_copy, nc.scalar.copy)[u]) for u in range(2)]
+        for u in range(2):
+            chans = slice(u * 2 * P, (u + 1) * 2 * P)
+            nc.vector.quantize_mx(out=last_codes[:, chans].bitcast(FP8X4), scales=last_scales[:, chans], in_=halves[u][:])
+        neg = [bounded_product(w3_q0, 0, u, fresh("neg_t", [P, BANK]), 1 + u) for u in range(2)]
         v_scales = held("v_scales", [P, S], U8)
         nc.vector.tensor_copy(v_scales[:], tab_plane[:, 0, :].indirect(offs_sb[:]))
-        corrections(0, 0, raw0[0:2], neg, g00)
-        g01 = weights(0, 1)
-        w3_q1 = []
-        for a in range(2):
-            w3_q1.append(quantize("w3_1%d" % a, group_w3(1, a, nc.scalar.copy)))
-        neg = [
-            bounded_product(w3_q0, 2 + a, w3_raw[1][a][:, 0, :].rearrange("p (t q) -> p t q", t=PACK)) for a in range(2)
-        ]
-        corrections(0, 1, raw0[2:4], neg, g01)
-        raw1 = [raw_product(1, jb) for jb in range(4)]
-        neg1 = [bounded_product(w3_q1, jb) for jb in range(4)]
+        place_pair(0, 0, 0, raw, neg[0], 0, squares())
+        place_pair(0, 0, 1, raw, neg[1], 5, squares())
+        neg = [bounded_product(w3_q0, 1, u, neg[1 - u], (3, 0)[u]) for u in range(2)]
+        place_pair(0, 1, 0, raw, neg[0], 6, squares())
+        w3_q1 = [quantize("w3_1%d" % a, deal(w3_raw[1][a], nc.scalar.copy)) for a in range(2)]
+        place_pair(0, 1, 1, raw, neg[1], 7, w3_raw[1][1][:, 0, :])
+        raw = [raw_product(1, jb, fresh("raw_t", [P, PACK, P]), (0, 5, 6, 7)[jb]) for jb in range(4)]
+        neg = [bounded_product(w3_q1, h, u, fresh("neg_t", [P, BANK]), 1 + 2 * h + u) for h in range(2) for u in range(2)]
 
         v_codes = held("v_codes", [P, S], I32)
         nc.vector.tensor_copy(v_codes[:].bitcast(U32), tab_sb[:].bitcast(U32).indirect(offs_sb[:]))
 
-        def group_w1(b):
-            grouped = staged("grouped", [P, PASS * PACK], BF16, 4)
-            nc.scalar.copy(
-                grouped[:].rearrange("p (t m i) -> p m i t", t=PACK, i=PACK),
-                w1_raw[b][:].rearrange("p i (m t) -> p m i t", t=PACK),
-            )
-            return grouped
-
-        g10 = weights(1, 0)
-        corrections(1, 0, raw1[0:2], neg1[0:2], g10)
-        w1_q = [quantize("w1_0", group_w1(0))]
-        g11 = weights(1, 1, w1_raw[0][:, 0:2, :].rearrange("p u (v j) -> p (u v) j", v=2))
-        corrections(1, 1, raw1[2:4], neg1[2:4], g11)
-        w1_q.append(quantize("w1_1", group_w1(1)))
+        place_pair(1, 0, 0, raw, neg[0], 0, squares())
+        place_pair(1, 0, 1, raw, neg[1], 5, squares())
+        w1_q = [quantize("w1_0", deal(w1_raw[0], nc.scalar.copy))]
+        place_pair(1, 1, 0, raw, neg[2], 6, w1_raw[0][:, 0, :])
+        place_pair(1, 1, 1, raw, neg[3], 7, w1_raw[0][:, 1, :])
+        w1_q.append(quantize("w1_1", deal(w1_raw[1], nc.scalar.copy)))
 
         def combine(b, c0, width, weave):
             cols = slice(c0, c0 + width)
             z = staged("z", [P, PACK, width], BF16, 2) if b == 0 else staged("sq", [P, PACK, width], BF16, 6)
             for t in range(PACK):
-                acc = bank("mx", 6)
+                acc = bank((1, 2, 3, 4)[t] if (c0 // width) % 2 == 0 else (0, 5, 6, 7)[t])
                 rows = slice(t * P, (t + 1) * P)
                 nc.tensor.matmul_mx(
                     out=acc[:, :width], lhsT=w1_q[b][0][:, rows].bitcast(FP8X4), lhsT_scale=w1_q[b][1][:, rows],
@@ -279,21 +283,31 @@ def tile_list_gloss_timing_features_kernel(
 
         z_grouped0 = [combine(0, half * BANK, BANK, nc.scalar.copy) for half in range(2)]
         chunks = [(0, 256), (256, 256), (512, 256), (768, 256)]
-        for half in range(2):
-            quantize_z(0, half * BANK, BANK, z_grouped0[half])
-        z_grouped1 = [combine(1, c0, width, nc.vector.tensor_copy if c0 == 768 else nc.scalar.copy) for c0, width in chunks]
-        for (c0, width), grouped in zip(chunks, z_grouped1):
+
+        def finish(index, grouped):
+            c0, width = chunks[index]
             quantize_z(1, c0, width, grouped)
             cols = slice(c0, c0 + width)
-            for nt in range(2):
-                acc = bank("mx", 6)
-                rows = slice(nt * P, (nt + 1) * P)
-                for b in range(2):
+            acc = bank((1, 0, 2, 5)[index])
+            for b in range(2):
+                for nt in range(2):
+                    rows = slice(nt * P, (nt + 1) * P)
                     nc.tensor.matmul_mx(
-                        out=acc[:, :width], lhsT=w4_sb[:, b, rows].bitcast(FP8X4), lhsT_scale=w4_plane[:, b, rows],
+                        out=acc[:, nt * width : (nt + 1) * width],
+                        lhsT=w4_sb[:, b, rows].bitcast(FP8X4), lhsT_scale=w4_plane[:, b, rows],
                         rhs=z_codes[b][:, cols].bitcast(FP8X4), rhs_scale=z_scales[b][:, cols],
-                        start=(b == 0), stop=(b == 1),
+                        start=(b == 0 and nt == 0), stop=(b == 1 and nt == 1),
                     )
-                res = staged(("raw_t", "neg_t")[nt], [P, width], F32, 4)
-                nc.scalar.activation(res[:], acc[:, :width], ACT.Sin, bias=zero[:])
-                nc.sync.dma_start(out[rows, cols], res[:])
+            res = staged("raw_t", [P, 2, width], F32, 4)
+            nc.scalar.activation(res[:].rearrange("p n j -> p (n j)"), acc[:, : 2 * width], ACT.Sin, bias=zero[:])
+            nc.sync.dma_start(out[:, cols].rearrange("(n p) j -> p n j", p=P), res[:])
+
+        for half in range(2):
+            quantize_z(0, half * BANK, BANK, z_grouped0[half])
+        z_grouped1 = []
+        for index, (c0, width) in enumerate(chunks):
+            z_grouped1.append(combine(1, c0, width, nc.vector.tensor_copy if index == 3 else nc.scalar.copy))
+            if index >= 2:
+                finish(index - 2, z_grouped1[index - 2])
+        finish(2, z_grouped1[2])
+        finish(3, z_grouped1[3])

@@ -43,6 +43,9 @@ def tile_list_gloss_timing_features_kernel(
         def staged(tag, shape, dtype, bufs):
             return ring.tile(shape, dtype, name=tag, tag=tag, bufs=bufs, align_bytes=64)
 
+        def tenant(tag, shape, dtype):
+            return ring.tile(shape, dtype, name=tag, tag=tag, bufs=1, align_bytes=64)
+
         def bank(n):
             return psum.tile([P, BANK], F32, name="bank%d" % n, tag="bank%d" % n)
 
@@ -87,7 +90,7 @@ def tile_list_gloss_timing_features_kernel(
         offs2_sb = lists.tile([P, PL // 16], U16, name="offs2_sb")
         pos_sb = lists.tile([P, PL // 16], U16, name="pos_sb")
         offs_sb = lists.tile([P, S // 16], U16, name="offs_sb")
-        tab2_sb = [held("tab2_sb%d" % a, [P, TB], I32) for a in range(2)]
+        tab2_sb = [held("tab2_sb0", [P, TB], I32), tenant("slot_a", [P, TB], I32)]
         w2_sb = [held("w2_sb%d" % b, [P, 2, 2 * PASS], U8) for b in range(2)]
         wgs_sb = held("wgs_sb", [P, PL], F32)
         gain_sb = held("gain_sb", [P, 2, PACK], F32)
@@ -121,8 +124,8 @@ def tile_list_gloss_timing_features_kernel(
         nc.sync.dma_start(pos_sb[:], pos1)
         load_w2_scales(1)
         w3_raw[1][0] = load_weight_rows(w3, 0, 1)
-        w3_raw[1][1] = load_weight_rows(w3, 1, 1)
         load_w2_words(1)
+        w3_raw[1][1] = load_weight_rows(w3, 1, 1)
         nc.sync.dma_start(tab_sb[:], tab_words[0].rearrange("p t i -> p (t i)").bitcast(I32))
         w1_raw = [load_weight_rows(w1, 0, 0)]
         nc.sync.dma_start(rest_sb[:], rest.rearrange("(b p t) -> p b t", b=2, t=PACK))
@@ -140,35 +143,36 @@ def tile_list_gloss_timing_features_kernel(
         spread = []
         for jb in range(4):
             tile = staged("neg_t", [P, PACK, QUADS, 32], F32, 4)
-            nc.vector.tensor_copy(
+            nc.scalar.copy(
                 tile[:],
                 wgs_t[:, jb * P : (jb + 1) * P].rearrange("j (q t) -> j t q", t=PACK).unsqueeze(2).to_broadcast([P, PACK, QUADS, 32]),
             )
             spread.append(tile)
-        weight = [held("weight%d" % b, [P, PACK, PL], F32) for b in range(2)]
-        for t in range(PACK):
-            dealt = bank(1 + t)
-            for jb in range(4):
-                nc.tensor.transpose(dealt[:, jb * P : (jb + 1) * P], spread[jb][:, t, :, :].rearrange("j u q -> j (u q)"), ident[:])
-            for b in range(2):
-                nc.scalar.activation(weight[b][:, t, :], dealt[:], ACT.Copy, scale=gain_sb[:, b, t : t + 1])
-
         v2_codes = []
         for a in range(2):
             codes = held("v2_codes%d" % a, [P, PL], I32)
             nc.vector.tensor_copy(codes[:].bitcast(U32), tab2_sb[a][:].bitcast(U32).indirect(offs2_sb[:]))
             v2_codes.append(codes)
 
-        def deal(raw, engine_copy):
-            grouped = staged("grouped", [P, PASS * PACK], BF16, 4)
+        weight = [held("weight0", [P, PACK, PL], F32), tenant("slot_a", [P, PACK, PL], F32)]
+        for t in range(PACK):
+            dealt = bank(1 + t)
+            for jb in range(4):
+                nc.tensor.transpose(dealt[:, jb * P : (jb + 1) * P], spread[jb][:, t, :, :].rearrange("j u q -> j (u q)"), ident[:])
+            nc.scalar.activation(weight[0][:, t, :], dealt[:], ACT.Copy, scale=gain_sb[:, 0, t : t + 1])
+            if t < 2:
+                nc.scalar.activation(weight[1][:, t, :], dealt[:], ACT.Copy, scale=gain_sb[:, 1, t : t + 1])
+            else:
+                nc.vector.tensor_scalar(weight[1][:, t, :], dealt[:], gain_sb[:, 1, t : t + 1], None, ALU.mult)
+
+        def deal(raw, engine_copy, grouped):
             engine_copy(
                 grouped[:].rearrange("p (t m i) -> p m i t", t=PACK, i=PACK),
                 raw[:].rearrange("p i (m t) -> p m i t", t=PACK),
             )
             return grouped
 
-        def deal_pair(raw, u, engine_copy):
-            grouped = staged("grouped", [P, 2 * P * PACK], BF16, 4)
+        def deal_pair(raw, u, engine_copy, grouped):
             engine_copy(
                 grouped[:].rearrange("p (e m i) -> p m i e", e=2, i=PACK),
                 raw[:].rearrange("p i (m u e) -> p u m i e", u=2, e=2)[:, u],
@@ -223,42 +227,55 @@ def tile_list_gloss_timing_features_kernel(
         def squares():
             return staged("sq", [P, BANK], F32, 6)[:]
 
-        raw = [raw_product(0, jb, fresh("raw_t", [P, PACK, P]), (0, 5, 6, 7)[jb]) for jb in range(4)]
-        w3_q0 = [quantize("w3_00", deal(w3_raw[0][0], nc.vector.tensor_copy))]
+        def any_grouped():
+            return staged("grouped", [P, PASS * PACK], BF16, 3)
+
+        raw_tiles = [fresh("raw_t", [P, PACK, P]), tenant("slot_b", [P, PACK, P], F32)[:], fresh("raw_t", [P, PACK, P]), fresh("raw_t", [P, PACK, P])]
+        raw = [raw_product(0, jb, raw_tiles[jb], (0, 5, 6, 7)[jb]) for jb in range(4)]
+        w3_q0 = [quantize("w3_00", deal(w3_raw[0][0], nc.vector.tensor_copy, any_grouped()))]
         last_codes = held("w3_01_codes", [P, PASS], I32)
         last_scales = held("w3_01_scales", [P, PASS], U8)
         w3_q0.append((last_codes, last_scales))
-        halves = [deal_pair(w3_raw[0][1], u, (nc.vector.tensor_copy, nc.scalar.copy)[u]) for u in range(2)]
+        halves = [
+            deal_pair(w3_raw[0][1], 0, nc.vector.tensor_copy, staged("grouped", [P, 2 * P * PACK], BF16, 3)),
+            deal_pair(w3_raw[0][1], 1, nc.scalar.copy, tenant("slot_c", [P, 2 * P * PACK], BF16)),
+        ]
         for u in range(2):
             chans = slice(u * 2 * P, (u + 1) * 2 * P)
             nc.vector.quantize_mx(out=last_codes[:, chans].bitcast(FP8X4), scales=last_scales[:, chans], in_=halves[u][:])
-        neg = [bounded_product(w3_q0, 0, u, fresh("neg_t", [P, BANK]), 1 + u) for u in range(2)]
-        v_scales = held("v_scales", [P, S], U8)
+        neg = [bounded_product(w3_q0, 0, u, fresh("neg_t", [P, BANK]), (0, 5)[u]) for u in range(2)]
+        v_scales = tenant("slot_c", [P, S], U8)
         nc.vector.tensor_copy(v_scales[:], tab_plane[:, 0, :].indirect(offs_sb[:]))
-        place_pair(0, 0, 0, raw, neg[0], 0, squares())
-        place_pair(0, 0, 1, raw, neg[1], 5, squares())
-        neg = [bounded_product(w3_q0, 1, u, neg[1 - u], (3, 0)[u]) for u in range(2)]
-        place_pair(0, 1, 0, raw, neg[0], 6, squares())
-        w3_q1 = [quantize("w3_1%d" % a, deal(w3_raw[1][a], nc.scalar.copy)) for a in range(2)]
-        place_pair(0, 1, 1, raw, neg[1], 7, w3_raw[1][1][:, 0, :])
-        raw = [raw_product(1, jb, fresh("raw_t", [P, PACK, P]), (0, 5, 6, 7)[jb]) for jb in range(4)]
-        neg = [bounded_product(w3_q1, h, u, fresh("neg_t", [P, BANK]), 1 + 2 * h + u) for h in range(2) for u in range(2)]
+        place_pair(0, 0, 0, raw, neg[0], 1, squares())
+        place_pair(0, 0, 1, raw, neg[1], 2, squares())
+        neg = [bounded_product(w3_q0, 1, u, neg[1 - u], (6, 1)[u]) for u in range(2)]
+        place_pair(0, 1, 0, raw, neg[0], 3, squares())
+        w3_q1 = [
+            quantize("w3_10", deal(w3_raw[1][0], nc.scalar.copy, tenant("slot_b", [P, PASS * PACK], BF16))),
+            quantize("w3_11", deal(w3_raw[1][1], nc.scalar.copy, tenant("slot_d", [P, PASS * PACK], BF16))),
+        ]
+        place_pair(0, 1, 1, raw, neg[1], 4, w3_raw[1][1][:, 0, :])
+        first_pair = tenant("slot_e", [P, 2, PACK, P], F32)
+        raw_tiles = [first_pair[:, 0], first_pair[:, 1], fresh("raw_t", [P, PACK, P]), fresh("raw_t", [P, PACK, P])]
+        raw = [raw_product(1, jb, raw_tiles[jb], (0, 5, 6, 7)[jb]) for jb in range(4)]
+        neg = [bounded_product(w3_q1, 0, u, fresh("neg_t", [P, BANK]), 6 + u) for u in range(2)]
 
-        v_codes = held("v_codes", [P, S], I32)
+        v_codes = tenant("slot_d", [P, S], I32)
         nc.vector.tensor_copy(v_codes[:].bitcast(U32), tab_sb[:].bitcast(U32).indirect(offs_sb[:]))
 
-        place_pair(1, 0, 0, raw, neg[0], 0, squares())
-        place_pair(1, 0, 1, raw, neg[1], 5, squares())
-        w1_q = [quantize("w1_0", deal(w1_raw[0], nc.scalar.copy))]
-        place_pair(1, 1, 0, raw, neg[2], 6, w1_raw[0][:, 0, :])
-        place_pair(1, 1, 1, raw, neg[3], 7, w1_raw[0][:, 1, :])
-        w1_q.append(quantize("w1_1", deal(w1_raw[1], nc.scalar.copy)))
+        place_pair(1, 0, 0, raw, neg[0], 1, squares())
+        place_pair(1, 0, 1, raw, neg[1], 2, squares())
+        neg = [bounded_product(w3_q1, 1, u, neg[1 - u], (0, 1)[u]) for u in range(2)]
+        w1_q = [quantize("w1_0", deal(w1_raw[0], nc.scalar.copy, tenant("slot_e", [P, PASS * PACK], BF16)))]
+        place_pair(1, 1, 0, raw, neg[0], 3, w1_raw[0][:, 0, :])
+        place_pair(1, 1, 1, raw, neg[1], 4, w1_raw[0][:, 1, :])
+        w1_q.append(quantize("w1_1", deal(w1_raw[1], nc.scalar.copy, tenant("slot_e", [P, PASS * PACK], BF16))))
 
         def combine(b, c0, width, weave):
             cols = slice(c0, c0 + width)
             z = staged("z", [P, PACK, width], BF16, 2) if b == 0 else staged("sq", [P, PACK, width], BF16, 6)
             for t in range(PACK):
-                acc = bank((1, 2, 3, 4)[t] if (c0 // width) % 2 == 0 else (0, 5, 6, 7)[t])
+                acc = bank((5, 6, 7, 0)[t] if (c0 // width) % 2 == 0 else (1, 2, 3, 4)[t])
                 rows = slice(t * P, (t + 1) * P)
                 nc.tensor.matmul_mx(
                     out=acc[:, :width], lhsT=w1_q[b][0][:, rows].bitcast(FP8X4), lhsT_scale=w1_q[b][1][:, rows],
@@ -267,7 +284,7 @@ def tile_list_gloss_timing_features_kernel(
                 nc.vector.scalar_tensor_tensor(
                     z[:, t, :], acc[:, :width], rest_sb[:, b, t : t + 1], pages[b][t][:, cols], ALU.max, ALU.add
                 )
-            grouped = staged("grouped", [P, width * PACK], BF16, 4) if b == 0 else staged("grouped1", [P, width * PACK], BF16, 4)
+            grouped = staged("grouped", [P, width * PACK], BF16, 3) if b == 0 else staged("grouped1", [P, width * PACK], BF16, 4)
             weave(
                 grouped[:].rearrange("p (c n t) -> p c t n", n=4, t=PACK),
                 z[:].rearrange("p t (c n) -> p c t n", n=4),
@@ -288,7 +305,7 @@ def tile_list_gloss_timing_features_kernel(
             c0, width = chunks[index]
             quantize_z(1, c0, width, grouped)
             cols = slice(c0, c0 + width)
-            acc = bank((1, 0, 2, 5)[index])
+            acc = bank((5, 1, 6, 2)[index])
             for b in range(2):
                 for nt in range(2):
                     rows = slice(nt * P, (nt + 1) * P)

@@ -20,10 +20,16 @@ ALU = mybir.AluOpType
 P = 128
 PACK = 4
 PASS = P * PACK
-QUADS = 4
+QUADS, QUAD = 4, 32
 QUAD_ORDER = (0, 2, 1, 3)
 BANK = 512
 PIECE = 256
+CHUNK = 256
+LIST_COLS = 16
+RING = 4
+GROUPED_RING = 3
+SQUARE_RING = 6
+WEIGHTS_ON_SCALAR = 2
 
 
 def tile_list_gloss_timing_features_kernel(
@@ -43,29 +49,14 @@ def tile_list_gloss_timing_features_kernel(
         def staged(tag, shape, dtype, bufs):
             return ring.tile(shape, dtype, name=tag, tag=tag, bufs=bufs, align_bytes=64)
 
-        def tenant(tag, shape, dtype):
-            return ring.tile(shape, dtype, name=tag, tag=tag, bufs=1, align_bytes=64)
+        def tenant(slot, shape, dtype):
+            return staged(slot, shape, dtype, 1)
 
         def bank(n):
             return psum.tile([P, BANK], F32, name="bank%d" % n, tag="bank%d" % n)
 
-        def load_scale_rows(plane, scales):
-            for q in QUAD_ORDER:
-                nc.sync.dma_start(
-                    plane[32 * q : 32 * q + 4, :, :].bitcast(I32),
-                    scales[:, 4 * q : 4 * q + 4, :].rearrange("a r c -> r a c").bitcast(I32),
-                )
-
-        def load_weight_rows(w, a, b):
-            raw = staged("w_raw", [P, PACK, PASS], F32, 4)
-            nc.sync.dma_start(raw[:], w[a * PASS : (a + 1) * PASS, b * PASS : (b + 1) * PASS].rearrange("(p i) c -> p i c", i=PACK))
-            return raw
-
-        def quantize(name, grouped):
-            codes = held(name + "_codes", [P, PASS], I32)
-            plane = held(name + "_scales", [P, PASS], U8)
-            nc.vector.quantize_mx(out=codes[:].bitcast(FP8X4), scales=plane[:], in_=grouped[:])
-            return codes, plane
+        def block(n):
+            return slice(n * P, (n + 1) * P)
 
         tab2_plane = held("tab2_plane", [P, 2, TB], U8)
         w2_plane = [held("w2_plane%d" % b, [P, 2, PASS], U8) for b in range(2)]
@@ -87,10 +78,10 @@ def tile_list_gloss_timing_features_kernel(
             for t in range(PACK):
                 nc.gpsimd.memset(pages[b][t][:], 0.0)
 
-        offs2_sb = lists.tile([P, PL // 16], U16, name="offs2_sb")
-        pos_sb = lists.tile([P, PL // 16], U16, name="pos_sb")
-        offs_sb = lists.tile([P, S // 16], U16, name="offs_sb")
-        tab2_sb = [held("tab2_sb0", [P, TB], I32), tenant("slot_a", [P, TB], I32)]
+        offs2_sb = lists.tile([P, PL // LIST_COLS], U16, name="offs2_sb")
+        pos_sb = lists.tile([P, PL // LIST_COLS], U16, name="pos_sb")
+        offs_sb = lists.tile([P, S // LIST_COLS], U16, name="offs_sb")
+        tab2_sb = [held("tab2_sb0", [P, TB], I32), tenant("after_tab2", [P, TB], I32)]
         w2_sb = [held("w2_sb%d" % b, [P, 2, 2 * PASS], U8) for b in range(2)]
         wgs_sb = held("wgs_sb", [P, PL], F32)
         gain_sb = held("gain_sb", [P, 2, PACK], F32)
@@ -98,38 +89,52 @@ def tile_list_gloss_timing_features_kernel(
         tab_sb = held("tab_sb", [P, T], I32)
         w4_sb = held("w4_sb", [P, 2, N], I32)
 
+        def load_scale_rows(plane, scales):
+            for q in QUAD_ORDER:
+                nc.sync.dma_start(
+                    plane[QUAD * q : QUAD * q + 4, :, :].bitcast(I32),
+                    scales[:, 4 * q : 4 * q + 4, :].rearrange("a r c -> r a c").bitcast(I32),
+                )
+
+        def load_table_words(tile, words):
+            nc.sync.dma_start(tile[:], words.rearrange("p t i -> p (t i)").bitcast(I32))
+
+        def load_weight_rows(w, a, b):
+            rows = staged("w_rows", [P, PACK, PASS], F32, RING)
+            nc.sync.dma_start(
+                rows[:], w[a * PASS : (a + 1) * PASS, b * PASS : (b + 1) * PASS].rearrange("(p i) c -> p i c", i=PACK)
+            )
+            return rows
+
         def load_w2_words(b):
             nc.sync.dma_start(
                 w2_sb[b][:].bitcast(I32),
                 w2_words[:, :, 2 * PASS * b : 2 * PASS * (b + 1)].rearrange("a p c -> p a c").bitcast(I32),
             )
 
-        def load_w2_scales(b):
-            cols = slice(b * PASS, (b + 1) * PASS)
-            load_scale_rows(w2_plane[b], w2_scales[:, :, cols])
+        def load_by_slice(tile, vector):
+            nc.sync.dma_start(tile[:], vector.rearrange("(b p t) -> p b t", b=2, t=PACK))
 
         nc.sync.dma_start(offs2_sb[:], offs2)
         nc.sync.dma_start(wgs_sb[:], wgs)
         load_scale_rows(tab2_plane, tab2_scales)
-        nc.sync.dma_start(tab2_sb[0][:], tab2_words[0].rearrange("p t i -> p (t i)").bitcast(I32))
-        nc.sync.dma_start(gain_sb[:], gain.rearrange("(b p t) -> p b t", b=2, t=PACK))
-        nc.sync.dma_start(tab2_sb[1][:], tab2_words[1].rearrange("p t i -> p (t i)").bitcast(I32))
-        w3_raw = [[None, None], [None, None]]
-        load_w2_scales(0)
+        load_table_words(tab2_sb[0], tab2_words[0])
+        load_by_slice(gain_sb, gain)
+        load_table_words(tab2_sb[1], tab2_words[1])
+        load_scale_rows(w2_plane[0], w2_scales[:, :, :PASS])
         load_w2_words(0)
-        w3_raw[0][0] = load_weight_rows(w3, 0, 0)
-        w3_raw[0][1] = load_weight_rows(w3, 1, 0)
+        w3_rows0 = [load_weight_rows(w3, a, 0) for a in range(2)]
         nc.sync.dma_start(offs_sb[:], offs)
         load_scale_rows(tab_plane, tab_scales)
         nc.sync.dma_start(pos_sb[:], pos1)
-        load_w2_scales(1)
-        w3_raw[1][0] = load_weight_rows(w3, 0, 1)
+        load_scale_rows(w2_plane[1], w2_scales[:, :, PASS:])
+        w3_rows1 = [load_weight_rows(w3, 0, 1)]
         load_w2_words(1)
-        w3_raw[1][1] = load_weight_rows(w3, 1, 1)
-        nc.sync.dma_start(tab_sb[:], tab_words[0].rearrange("p t i -> p (t i)").bitcast(I32))
-        w1_raw = [load_weight_rows(w1, 0, 0)]
-        nc.sync.dma_start(rest_sb[:], rest.rearrange("(b p t) -> p b t", b=2, t=PACK))
-        w1_raw.append(load_weight_rows(w1, 0, 1))
+        w3_rows1.append(load_weight_rows(w3, 1, 1))
+        load_table_words(tab_sb, tab_words[0])
+        w1_rows = [load_weight_rows(w1, 0, 0)]
+        load_by_slice(rest_sb, rest)
+        w1_rows.append(load_weight_rows(w1, 0, 1))
         nc.sync.dma_start(w4_sb[:], w4_words.rearrange("a p c i -> p a (c i)").bitcast(I32))
         load_scale_rows(w4_plane, w4_scales)
 
@@ -138,53 +143,63 @@ def tile_list_gloss_timing_features_kernel(
             nc.vector.tensor_copy(v2_scales[a][:], tab2_plane[:, a, :].indirect(offs2_sb[:]))
 
         wgs_t = bank(0)
-        for jb in range(4):
-            nc.tensor.transpose(wgs_t[:, jb * P : (jb + 1) * P], wgs_sb[:, jb * P : (jb + 1) * P], ident[:])
+        for jb in range(PL // P):
+            nc.tensor.transpose(wgs_t[:, block(jb)], wgs_sb[:, block(jb)], ident[:])
         spread = []
-        for jb in range(4):
-            tile = staged("neg_t", [P, PACK, QUADS, 32], F32, 4)
-            nc.scalar.copy(
-                tile[:],
-                wgs_t[:, jb * P : (jb + 1) * P].rearrange("j (q t) -> j t q", t=PACK).unsqueeze(2).to_broadcast([P, PACK, QUADS, 32]),
-            )
-            spread.append(tile)
+        for jb in range(PL // P):
+            repeated = staged("scalar_out", [P, PACK, QUADS, QUAD], F32, RING)
+            by_slice = wgs_t[:, block(jb)].rearrange("j (q t) -> j t q", t=PACK)
+            nc.scalar.copy(repeated[:], by_slice.unsqueeze(2).to_broadcast([P, PACK, QUADS, QUAD]))
+            spread.append(repeated)
+
         v2_codes = []
         for a in range(2):
             codes = held("v2_codes%d" % a, [P, PL], I32)
             nc.vector.tensor_copy(codes[:].bitcast(U32), tab2_sb[a][:].bitcast(U32).indirect(offs2_sb[:]))
             v2_codes.append(codes)
 
-        weight = [held("weight0", [P, PACK, PL], F32), tenant("slot_a", [P, PACK, PL], F32)]
+        weight = [held("weight0", [P, PACK, PL], F32), tenant("after_tab2", [P, PACK, PL], F32)]
         for t in range(PACK):
             dealt = bank(1 + t)
-            for jb in range(4):
-                nc.tensor.transpose(dealt[:, jb * P : (jb + 1) * P], spread[jb][:, t, :, :].rearrange("j u q -> j (u q)"), ident[:])
+            for jb in range(PL // P):
+                nc.tensor.transpose(dealt[:, block(jb)], spread[jb][:, t, :, :].rearrange("j u q -> j (u q)"), ident[:])
             nc.scalar.activation(weight[0][:, t, :], dealt[:], ACT.Copy, scale=gain_sb[:, 0, t : t + 1])
-            if t < 2:
+            if t < WEIGHTS_ON_SCALAR:
                 nc.scalar.activation(weight[1][:, t, :], dealt[:], ACT.Copy, scale=gain_sb[:, 1, t : t + 1])
             else:
                 nc.vector.tensor_scalar(weight[1][:, t, :], dealt[:], gain_sb[:, 1, t : t + 1], None, ALU.mult)
 
-        def deal(raw, engine_copy, grouped):
+        def deal(rows, engine_copy, grouped):
             engine_copy(
                 grouped[:].rearrange("p (t m i) -> p m i t", t=PACK, i=PACK),
-                raw[:].rearrange("p i (m t) -> p m i t", t=PACK),
+                rows[:].rearrange("p i (m t) -> p m i t", t=PACK),
             )
             return grouped
 
-        def deal_pair(raw, u, engine_copy, grouped):
+        def deal_pair(rows, u, engine_copy, grouped):
             engine_copy(
                 grouped[:].rearrange("p (e m i) -> p m i e", e=2, i=PACK),
-                raw[:].rearrange("p i (m u e) -> p u m i e", u=2, e=2)[:, u],
+                rows[:].rearrange("p i (m u e) -> p u m i e", u=2, e=2)[:, u],
             )
             return grouped
+
+        def next_grouped(columns):
+            return staged("grouped", [P, columns * PACK], BF16, GROUPED_RING)
+
+        def quantize(codes, scales, grouped):
+            nc.vector.quantize_mx(out=codes.bitcast(FP8X4), scales=scales, in_=grouped[:])
+
+        def quantized(name, grouped):
+            codes = held(name + "_codes", [P, PASS], I32)
+            scales = held(name + "_scales", [P, PASS], U8)
+            quantize(codes[:], scales[:], grouped)
+            return codes, scales
 
         def raw_product(b, jb, raw_t, n):
             acc = bank(n)
-            cols = slice(jb * P, (jb + 1) * P)
             for a in range(2):
                 nc.tensor.matmul_mx(
-                    out=acc[:], lhsT=v2_codes[a][:, cols].bitcast(FP8X4), lhsT_scale=v2_scales[a][:, cols],
+                    out=acc[:], lhsT=v2_codes[a][:, block(jb)].bitcast(FP8X4), lhsT_scale=v2_scales[a][:, block(jb)],
                     rhs=w2_sb[b][:, a, :].bitcast(FP4X4), rhs_scale=w2_plane[b][:, a, :],
                     start=(a == 0), stop=(a == 1),
                 )
@@ -196,135 +211,171 @@ def tile_list_gloss_timing_features_kernel(
             chans = slice(u * 2 * P, (u + 1) * 2 * P)
             for a in range(2):
                 for e in range(2):
-                    cols = slice((2 * h + e) * P, (2 * h + e + 1) * P)
+                    entries = block(2 * h + e)
                     nc.tensor.matmul_mx(
                         out=acc[:, e * 2 * P : (e + 1) * 2 * P],
-                        lhsT=v2_codes[a][:, cols].bitcast(FP8X4), lhsT_scale=v2_scales[a][:, cols],
+                        lhsT=v2_codes[a][:, entries].bitcast(FP8X4), lhsT_scale=v2_scales[a][:, entries],
                         rhs=w3_q[a][0][:, chans].bitcast(FP8X4), rhs_scale=w3_q[a][1][:, chans],
                         start=(a == 0 and e == 0), stop=(a == 1 and e == 1),
                     )
             nc.scalar.activation(neg_t, acc[:], ACT.Tanh, bias=zero[:], scale=-1.0)
             return neg_t
 
-        def fresh(tag, shape):
-            return staged(tag, shape, F32, 4)[:]
-
-        def place_pair(b, h, u, raw_ts, neg_t, n, sq):
+        def place(b, h, u, raw_ts, neg_t, n, square):
             diff = bank(n)
             for v in range(2):
                 for e in range(2):
-                    dst = diff[:, v * PIECE + e * P : v * PIECE + (e + 1) * P]
-                    nc.tensor.matmul(dst, neg_t[:, (2 * e + v) * P : (2 * e + v + 1) * P], ident[:], start=True, stop=False, is_transpose=True)
-                    nc.tensor.matmul(dst, raw_ts[2 * h + e][:, 2 * u + v, :], ident[:], start=False, stop=True, is_transpose=True)
-            nc.scalar.activation(sq, diff[:], ACT.Square, bias=zero[:])
+                    dst = diff[:, block(2 * v + e)]
+                    nc.tensor.matmul(dst, neg_t[:, block(2 * e + v)], ident[:], start=True, stop=False, is_transpose=True)
+                    nc.tensor.matmul(
+                        dst, raw_ts[2 * h + e][:, 2 * u + v, :], ident[:], start=False, stop=True, is_transpose=True
+                    )
+            nc.scalar.activation(square, diff[:], ACT.Square, bias=zero[:])
+            offsets = pos_sb[:, h * PIECE // LIST_COLS : (h + 1) * PIECE // LIST_COLS]
             for v in range(2):
                 t = 2 * u + v
                 nc.vector.tensor_tensor(
-                    pages[b][t][:].indirect(pos_sb[:, h * (PIECE // 16) : (h + 1) * (PIECE // 16)]),
-                    sq[:, v * PIECE : (v + 1) * PIECE], weight[b][:, t, h * PIECE : (h + 1) * PIECE], ALU.mult,
+                    pages[b][t][:].indirect(offsets),
+                    square[:, v * PIECE : (v + 1) * PIECE], weight[b][:, t, h * PIECE : (h + 1) * PIECE], ALU.mult,
                 )
 
-        def squares():
-            return staged("sq", [P, BANK], F32, 6)[:]
+        def next_raw():
+            return staged("raw_t", [P, PACK, P], F32, RING)[:]
 
-        def any_grouped():
-            return staged("grouped", [P, PASS * PACK], BF16, 3)
+        def next_scalar_out():
+            return staged("scalar_out", [P, BANK], F32, RING)[:]
 
-        raw_tiles = [fresh("raw_t", [P, PACK, P]), tenant("slot_b", [P, PACK, P], F32)[:], fresh("raw_t", [P, PACK, P]), fresh("raw_t", [P, PACK, P])]
-        raw = [raw_product(0, jb, raw_tiles[jb], (0, 5, 6, 7)[jb]) for jb in range(4)]
-        w3_q0 = [quantize("w3_00", deal(w3_raw[0][0], nc.vector.tensor_copy, any_grouped()))]
-        last_codes = held("w3_01_codes", [P, PASS], I32)
-        last_scales = held("w3_01_scales", [P, PASS], U8)
-        w3_q0.append((last_codes, last_scales))
+        def next_square():
+            return staged("square", [P, BANK], F32, SQUARE_RING)[:]
+
+        raw_banks = (0, 5, 6, 7)
+        raw_tiles = [next_raw(), tenant("after_first_half", [P, PACK, P], F32)[:], next_raw(), next_raw()]
+        raw = [raw_product(0, jb, raw_tiles[jb], raw_banks[jb]) for jb in range(PL // P)]
+        w3_q0 = [quantized("w3_00", deal(w3_rows0[0], nc.vector.tensor_copy, next_grouped(PASS)))]
+        w3_q0.append((held("w3_01_codes", [P, PASS], I32), held("w3_01_scales", [P, PASS], U8)))
         halves = [
-            deal_pair(w3_raw[0][1], 0, nc.vector.tensor_copy, staged("grouped", [P, 2 * P * PACK], BF16, 3)),
-            deal_pair(w3_raw[0][1], 1, nc.scalar.copy, tenant("slot_c", [P, 2 * P * PACK], BF16)),
+            deal_pair(w3_rows0[1], 0, nc.vector.tensor_copy, next_grouped(2 * P)),
+            deal_pair(w3_rows0[1], 1, nc.scalar.copy, tenant("after_w3_01", [P, 2 * P * PACK], BF16)),
         ]
         for u in range(2):
             chans = slice(u * 2 * P, (u + 1) * 2 * P)
-            nc.vector.quantize_mx(out=last_codes[:, chans].bitcast(FP8X4), scales=last_scales[:, chans], in_=halves[u][:])
-        neg = [bounded_product(w3_q0, 0, u, fresh("neg_t", [P, BANK]), (0, 5)[u]) for u in range(2)]
-        v_scales = tenant("slot_c", [P, S], U8)
+            quantize(w3_q0[1][0][:, chans], w3_q0[1][1][:, chans], halves[u])
+        neg = [bounded_product(w3_q0, 0, u, next_scalar_out(), raw_banks[u]) for u in range(2)]
+        v_scales = tenant("after_w3_01", [P, S], U8)
         nc.vector.tensor_copy(v_scales[:], tab_plane[:, 0, :].indirect(offs_sb[:]))
-        place_pair(0, 0, 0, raw, neg[0], 1, squares())
-        place_pair(0, 0, 1, raw, neg[1], 2, squares())
-        neg = [bounded_product(w3_q0, 1, u, neg[1 - u], (6, 1)[u]) for u in range(2)]
-        place_pair(0, 1, 0, raw, neg[0], 3, squares())
+        place(0, 0, 0, raw, neg[0], 1, next_square())
+        place(0, 0, 1, raw, neg[1], 2, next_square())
+        neg = [bounded_product(w3_q0, 1, 0, neg[1], raw_banks[2]), bounded_product(w3_q0, 1, 1, neg[0], 1)]
+        place(0, 1, 0, raw, neg[0], 3, next_square())
         w3_q1 = [
-            quantize("w3_10", deal(w3_raw[1][0], nc.scalar.copy, tenant("slot_b", [P, PASS * PACK], BF16))),
-            quantize("w3_11", deal(w3_raw[1][1], nc.scalar.copy, tenant("slot_d", [P, PASS * PACK], BF16))),
+            quantized("w3_10", deal(w3_rows1[0], nc.scalar.copy, tenant("after_first_half", [P, PASS * PACK], BF16))),
+            quantized("w3_11", deal(w3_rows1[1], nc.scalar.copy, tenant("after_w3_11", [P, PASS * PACK], BF16))),
         ]
-        place_pair(0, 1, 1, raw, neg[1], 4, w3_raw[1][1][:, 0, :])
-        first_pair = tenant("slot_e", [P, 2, PACK, P], F32)
-        raw_tiles = [first_pair[:, 0], first_pair[:, 1], fresh("raw_t", [P, PACK, P]), fresh("raw_t", [P, PACK, P])]
-        raw = [raw_product(1, jb, raw_tiles[jb], (0, 5, 6, 7)[jb]) for jb in range(4)]
-        neg = [bounded_product(w3_q1, 0, u, fresh("neg_t", [P, BANK]), 6 + u) for u in range(2)]
+        place(0, 1, 1, raw, neg[1], 4, w3_rows1[1][:, 0, :])
 
-        v_codes = tenant("slot_d", [P, S], I32)
+        first_raw = tenant("after_third_half", [P, 2, PACK, P], F32)
+        spent_rows = w3_rows1[1][:].rearrange("j i (t p) -> j i t p", t=PACK)
+        raw_tiles = [first_raw[:, 0], first_raw[:, 1], spent_rows[:, 1], spent_rows[:, 2]]
+        raw = [raw_product(1, jb, raw_tiles[jb], raw_banks[jb]) for jb in range(PL // P)]
+        neg = [bounded_product(w3_q1, 0, u, next_scalar_out(), raw_banks[2 + u]) for u in range(2)]
+        v_codes = tenant("after_w3_11", [P, S], I32)
         nc.vector.tensor_copy(v_codes[:].bitcast(U32), tab_sb[:].bitcast(U32).indirect(offs_sb[:]))
+        place(1, 0, 0, raw, neg[0], 1, next_square())
+        w1_q = [quantized("w1_0", deal(w1_rows[0], nc.scalar.copy, tenant("after_third_half", [P, PASS * PACK], BF16)))]
+        place(1, 0, 1, raw, neg[1], 2, w1_rows[0][:, 0, :])
+        neg = [bounded_product(w3_q1, 1, 0, neg[1], raw_banks[0]), bounded_product(w3_q1, 1, 1, neg[0], 1)]
+        place(1, 1, 0, raw, neg[0], 3, next_square())
+        place(1, 1, 1, raw, neg[1], 4, next_square())
 
-        place_pair(1, 0, 0, raw, neg[0], 1, squares())
-        place_pair(1, 0, 1, raw, neg[1], 2, squares())
-        neg = [bounded_product(w3_q1, 1, u, neg[1 - u], (0, 1)[u]) for u in range(2)]
-        w1_q = [quantize("w1_0", deal(w1_raw[0], nc.scalar.copy, tenant("slot_e", [P, PASS * PACK], BF16)))]
-        place_pair(1, 1, 0, raw, neg[0], 3, w1_raw[0][:, 0, :])
-        place_pair(1, 1, 1, raw, neg[1], 4, w1_raw[0][:, 1, :])
-        w1_q.append(quantize("w1_1", deal(w1_raw[1], nc.scalar.copy, tenant("slot_e", [P, PASS * PACK], BF16))))
+        def gloss_product(b, t, cols, acc):
+            nc.tensor.matmul_mx(
+                out=acc, lhsT=w1_q[b][0][:, block(t)].bitcast(FP8X4), lhsT_scale=w1_q[b][1][:, block(t)],
+                rhs=v_codes[:, cols].bitcast(FP8X4), rhs_scale=v_scales[:, cols], start=True, stop=True,
+            )
 
-        def combine(b, c0, width, weave):
-            cols = slice(c0, c0 + width)
-            z = staged("z", [P, PACK, width], BF16, 2) if b == 0 else staged("sq", [P, PACK, width], BF16, 6)
+        def combine_without_vector():
+            gloss_banks = (3, 4, 1, 2)
+            sum_banks = (5, 6)
+            gloss, lift = [], []
             for t in range(PACK):
-                acc = bank((5, 6, 7, 0)[t] if (c0 // width) % 2 == 0 else (1, 2, 3, 4)[t])
-                rows = slice(t * P, (t + 1) * P)
-                nc.tensor.matmul_mx(
-                    out=acc[:, :width], lhsT=w1_q[b][0][:, rows].bitcast(FP8X4), lhsT_scale=w1_q[b][1][:, rows],
-                    rhs=v_codes[:, cols].bitcast(FP8X4), rhs_scale=v_scales[:, cols], start=True, stop=True,
-                )
+                acc = bank(gloss_banks[t])[:, :CHUNK]
+                gloss_product(0, t, slice(0, CHUNK), acc)
+                gloss.append(staged("raw_t", [P, CHUNK], F32, RING)[:])
+                nc.scalar.copy(gloss[t], acc)
+                lift.append(staged("scalar_out", [P, CHUNK], F32, RING)[:])
+                nc.scalar.activation(lift[t], acc, ACT.Relu, bias=rest_sb[:, 0, t : t + 1], scale=-1.0)
+            grouped = next_grouped(CHUNK)
+            back = bank(gloss_banks[0])
+            for jb in range(CHUNK // P):
+                total = bank(sum_banks[jb])
+                for t in range(PACK):
+                    for k, term in enumerate((gloss[t], pages[0][t], lift[t])):
+                        nc.tensor.matmul(
+                            total[:, block(t)], term[:, block(jb)], ident[:],
+                            start=(k == 0), stop=(k == 2), is_transpose=True,
+                        )
+                z_t = tenant("z_t%d" % jb, [P, 2, P, 2], BF16)
+                nc.scalar.copy(z_t[:], total[:].rearrange("j (u v p) -> j u p v", u=2, v=2))
+                pairs = z_t[:].rearrange("j u p v -> j (u p v)").bitcast(F32)
+                for u in range(2):
+                    nc.tensor.transpose(back[:, block(2 * jb + u)], pairs[:, block(u)], ident[:])
+            words = grouped[:].bitcast(F32).rearrange("p (e j u) -> p e j u", e=2, u=2)
+            nc.scalar.copy(words, back[:].rearrange("p (e u j) -> p e j u", e=2, u=2))
+            return grouped
+
+        def combine(b, c0, z, banks, weave, grouped):
+            width = z.shape[2]
+            cols = slice(c0, c0 + width)
+            for t in range(PACK):
+                acc = bank(banks[t])
+                gloss_product(b, t, cols, acc[:, :width])
                 nc.vector.scalar_tensor_tensor(
                     z[:, t, :], acc[:, :width], rest_sb[:, b, t : t + 1], pages[b][t][:, cols], ALU.max, ALU.add
                 )
-            grouped = staged("grouped", [P, width * PACK], BF16, 3) if b == 0 else staged("grouped1", [P, width * PACK], BF16, 4)
             weave(
                 grouped[:].rearrange("p (c n t) -> p c t n", n=4, t=PACK),
                 z[:].rearrange("p t (c n) -> p c t n", n=4),
             )
             return grouped
 
+        z_first = combine_without_vector()
+        w1_last = deal(w1_rows[1], nc.scalar.copy, tenant("after_third_half", [P, PASS * PACK], BF16))
+        w1_q.append((tenant("z_t1", [P, PASS], I32), held("w1_1_scales", [P, PASS], U8)))
+        quantize(w1_q[1][0][:], w1_q[1][1][:], w1_last)
+
         z_codes = [held("z_codes%d" % b, [P, S], I32) for b in range(2)]
         z_scales = [held("z_scales%d" % b, [P, S], U8) for b in range(2)]
+        bank_sets = ((1, 2, 5, 3), (7, 0, 4, 6))
+        z_second = combine(0, CHUNK, held("z_second", [P, PACK, CHUNK], BF16), bank_sets[1], nc.scalar.copy, next_grouped(CHUNK))
+        z_third = combine(0, BANK, held("z_third", [P, PACK, BANK], BF16), bank_sets[0], nc.scalar.copy, next_grouped(BANK))
+        for cols, grouped in ((slice(0, CHUNK), z_first), (slice(CHUNK, BANK), z_second), (slice(BANK, S), z_third)):
+            quantize(z_codes[0][:, cols], z_scales[0][:, cols], grouped)
 
-        def quantize_z(b, c0, width, grouped):
-            cols = slice(c0, c0 + width)
-            nc.vector.quantize_mx(out=z_codes[b][:, cols].bitcast(FP8X4), scales=z_scales[b][:, cols], in_=grouped[:])
-
-        z_grouped0 = [combine(0, half * BANK, BANK, nc.scalar.copy) for half in range(2)]
-        chunks = [(0, 256), (256, 256), (512, 256), (768, 256)]
+        chunks = S // CHUNK
 
         def finish(index, grouped):
-            c0, width = chunks[index]
-            quantize_z(1, c0, width, grouped)
-            cols = slice(c0, c0 + width)
-            acc = bank((5, 1, 6, 2)[index])
+            cols = slice(index * CHUNK, (index + 1) * CHUNK)
+            quantize(z_codes[1][:, cols], z_scales[1][:, cols], grouped)
+            acc = bank(bank_sets[(index + 1) % 2][index // 2])
             for b in range(2):
-                for nt in range(2):
-                    rows = slice(nt * P, (nt + 1) * P)
+                for nt in range(N // P):
                     nc.tensor.matmul_mx(
-                        out=acc[:, nt * width : (nt + 1) * width],
-                        lhsT=w4_sb[:, b, rows].bitcast(FP8X4), lhsT_scale=w4_plane[:, b, rows],
+                        out=acc[:, nt * CHUNK : (nt + 1) * CHUNK],
+                        lhsT=w4_sb[:, b, block(nt)].bitcast(FP8X4), lhsT_scale=w4_plane[:, b, block(nt)],
                         rhs=z_codes[b][:, cols].bitcast(FP8X4), rhs_scale=z_scales[b][:, cols],
-                        start=(b == 0 and nt == 0), stop=(b == 1 and nt == 1),
+                        start=(b == 0 and nt == 0), stop=(b == 1 and nt == N // P - 1),
                     )
-            res = staged("raw_t", [P, 2, width], F32, 4)
-            nc.scalar.activation(res[:].rearrange("p n j -> p (n j)"), acc[:, : 2 * width], ACT.Sin, bias=zero[:])
-            nc.sync.dma_start(out[:, cols].rearrange("(n p) j -> p n j", p=P), res[:])
+            features = staged("raw_t", [P, N // P, CHUNK], F32, RING)
+            nc.scalar.activation(features[:].rearrange("p n j -> p (n j)"), acc[:], ACT.Sin, bias=zero[:])
+            nc.sync.dma_start(out[:, cols].rearrange("(n p) j -> p n j", p=P), features[:])
 
-        for half in range(2):
-            quantize_z(0, half * BANK, BANK, z_grouped0[half])
-        z_grouped1 = []
-        for index, (c0, width) in enumerate(chunks):
-            z_grouped1.append(combine(1, c0, width, nc.vector.tensor_copy if index == 3 else nc.scalar.copy))
+        woven = []
+        for index in range(chunks):
+            weave = nc.vector.tensor_copy if index == chunks - 1 else nc.scalar.copy
+            z = staged("square", [P, PACK, CHUNK], BF16, SQUARE_RING)
+            grouped = staged("chunk_grouped", [P, CHUNK * PACK], BF16, chunks)
+            woven.append(combine(1, index * CHUNK, z, bank_sets[(index + 1) % 2], weave, grouped))
             if index >= 2:
-                finish(index - 2, z_grouped1[index - 2])
-        finish(2, z_grouped1[2])
-        finish(3, z_grouped1[3])
+                finish(index - 2, woven[index - 2])
+        for index in range(chunks - 2, chunks):
+            finish(index, woven[index])

from contextlib import ExitStack

import concourse.mybir as mybir
from concourse.masks import make_identity

K, K2, H, N, T, TB, S, PL = 512, 1024, 1024, 256, 4096, 2048, 1024, 512
FLOPS = 2 * (K * H * S + 2 * K2 * H * PL + H * N * S)

F32 = mybir.dt.float32
BF16 = mybir.dt.bfloat16
I32 = mybir.dt.int32
U32 = mybir.dt.uint32
U16 = mybir.dt.uint16
U8 = mybir.dt.uint8
FP8X4 = mybir.dt.float8_e4m3fn_x4
FP4X4 = mybir.dt.float4_e2m1fn_x4
ACT = mybir.ActivationFunctionType
ALU = mybir.AluOpType

P = 128
PACK = 4
PASS = P * PACK
QUADS, QUAD = 4, 32
QUAD_ORDER = (0, 2, 1, 3)
BANK = 512
PIECE = 256
CHUNK = 256
LIST_COLS = 16
RING = 4
GROUPED_RING = 3
SQUARE_RING = 6
WEIGHTS_ON_SCALAR = 2


def tile_list_gloss_timing_features_kernel(
    tc, tab_words, tab_scales, tab2_words, tab2_scales, offs, offs2, pos1, w1, rest, w2_words, w2_scales, w3, gain, wgs,
    w4_words, w4_scales, out,
):
    nc = tc.nc
    with ExitStack() as ctx:
        lists = ctx.enter_context(tc.tile_pool(name="lists", bufs=1))
        keep = ctx.enter_context(tc.tile_pool(name="keep", bufs=1))
        ring = ctx.enter_context(tc.tile_pool(name="ring", bufs=1))
        psum = ctx.enter_context(tc.psum_pool(name="psum", bufs=1))

        def held(name, shape, dtype):
            return keep.tile(shape, dtype, name=name, align_bytes=64)

        def staged(tag, shape, dtype, bufs):
            return ring.tile(shape, dtype, name=tag, tag=tag, bufs=bufs, align_bytes=64)

        def tenant(slot, shape, dtype):
            return staged(slot, shape, dtype, 1)

        def bank(n):
            return psum.tile([P, BANK], F32, name="bank%d" % n, tag="bank%d" % n)

        def block(n):
            return slice(n * P, (n + 1) * P)

        tab2_plane = held("tab2_plane", [P, 2, TB], U8)
        w2_plane = [held("w2_plane%d" % b, [P, 2, PASS], U8) for b in range(2)]
        tab_plane = held("tab_plane", [P, 1, T], U8)
        w4_plane = held("w4_plane", [P, 2, N], U8)
        zero_in = held("zero_in", [P, 1], F32)
        zero = held("zero", [P, 1], F32)
        nc.vector.memset(tab2_plane[:].bitcast(I32), 0)
        nc.vector.memset(w2_plane[0][:].bitcast(I32), 0)
        nc.vector.memset(zero_in[:], 0.0)
        nc.scalar.activation(zero[:], zero_in[:], ACT.Silu)
        nc.vector.memset(tab_plane[:].bitcast(I32), 0)
        nc.vector.memset(w2_plane[1][:].bitcast(I32), 0)
        ident = held("ident", [P, P], F32)
        make_identity(nc, ident[:])
        nc.gpsimd.memset(w4_plane[:].bitcast(I32), 0)
        pages = [[held("page%d%d" % (b, t), [P, S], F32) for t in range(PACK)] for b in range(2)]
        for b in range(2):
            for t in range(PACK):
                nc.gpsimd.memset(pages[b][t][:], 0.0)

        offs2_sb = lists.tile([P, PL // LIST_COLS], U16, name="offs2_sb")
        pos_sb = lists.tile([P, PL // LIST_COLS], U16, name="pos_sb")
        offs_sb = lists.tile([P, S // LIST_COLS], U16, name="offs_sb")
        tab2_sb = [held("tab2_sb0", [P, TB], I32), tenant("after_tab2", [P, TB], I32)]
        w2_sb = [held("w2_sb%d" % b, [P, 2, 2 * PASS], U8) for b in range(2)]
        wgs_sb = held("wgs_sb", [P, PL], F32)
        gain_sb = held("gain_sb", [P, 2, PACK], F32)
        rest_sb = held("rest_sb", [P, 2, PACK], F32)
        tab_sb = held("tab_sb", [P, T], I32)
        w4_sb = held("w4_sb", [P, 2, N], I32)

        def load_scale_rows(plane, scales):
            for q in QUAD_ORDER:
                nc.sync.dma_start(
                    plane[QUAD * q : QUAD * q + 4, :, :].bitcast(I32),
                    scales[:, 4 * q : 4 * q + 4, :].rearrange("a r c -> r a c").bitcast(I32),
                )

        def load_table_words(tile, words):
            nc.sync.dma_start(tile[:], words.rearrange("p t i -> p (t i)").bitcast(I32))

        def load_weight_rows(w, a, b):
            rows = staged("w_rows", [P, PACK, PASS], F32, RING)
            nc.sync.dma_start(
                rows[:], w[a * PASS : (a + 1) * PASS, b * PASS : (b + 1) * PASS].rearrange("(p i) c -> p i c", i=PACK)
            )
            return rows

        def load_w2_words(b):
            nc.sync.dma_start(
                w2_sb[b][:].bitcast(I32),
                w2_words[:, :, 2 * PASS * b : 2 * PASS * (b + 1)].rearrange("a p c -> p a c").bitcast(I32),
            )

        def load_by_slice(tile, vector):
            nc.sync.dma_start(tile[:], vector.rearrange("(b p t) -> p b t", b=2, t=PACK))

        nc.sync.dma_start(offs2_sb[:], offs2)
        nc.sync.dma_start(wgs_sb[:], wgs)
        load_scale_rows(tab2_plane, tab2_scales)
        load_table_words(tab2_sb[0], tab2_words[0])
        load_by_slice(gain_sb, gain)
        load_table_words(tab2_sb[1], tab2_words[1])
        load_scale_rows(w2_plane[0], w2_scales[:, :, :PASS])
        load_w2_words(0)
        w3_rows0 = [load_weight_rows(w3, a, 0) for a in range(2)]
        nc.sync.dma_start(offs_sb[:], offs)
        load_scale_rows(tab_plane, tab_scales)
        nc.sync.dma_start(pos_sb[:], pos1)
        load_scale_rows(w2_plane[1], w2_scales[:, :, PASS:])
        w3_rows1 = [load_weight_rows(w3, 0, 1)]
        load_w2_words(1)
        w3_rows1.append(load_weight_rows(w3, 1, 1))
        load_table_words(tab_sb, tab_words[0])
        w1_rows = [load_weight_rows(w1, 0, 0)]
        load_by_slice(rest_sb, rest)
        w1_rows.append(load_weight_rows(w1, 0, 1))
        nc.sync.dma_start(w4_sb[:], w4_words.rearrange("a p c i -> p a (c i)").bitcast(I32))
        load_scale_rows(w4_plane, w4_scales)

        v2_scales = [held("v2_scales%d" % a, [P, PL], U8) for a in range(2)]
        for a in range(2):
            nc.vector.tensor_copy(v2_scales[a][:], tab2_plane[:, a, :].indirect(offs2_sb[:]))

        wgs_t = bank(0)
        for jb in range(PL // P):
            nc.tensor.transpose(wgs_t[:, block(jb)], wgs_sb[:, block(jb)], ident[:])
        spread = []
        for jb in range(PL // P):
            repeated = staged("scalar_out", [P, PACK, QUADS, QUAD], F32, RING)
            by_slice = wgs_t[:, block(jb)].rearrange("j (q t) -> j t q", t=PACK)
            nc.scalar.copy(repeated[:], by_slice.unsqueeze(2).to_broadcast([P, PACK, QUADS, QUAD]))
            spread.append(repeated)

        v2_codes = []
        for a in range(2):
            codes = held("v2_codes%d" % a, [P, PL], I32)
            nc.vector.tensor_copy(codes[:].bitcast(U32), tab2_sb[a][:].bitcast(U32).indirect(offs2_sb[:]))
            v2_codes.append(codes)

        weight = [held("weight0", [P, PACK, PL], F32), tenant("after_tab2", [P, PACK, PL], F32)]
        for t in range(PACK):
            dealt = bank(1 + t)
            for jb in range(PL // P):
                nc.tensor.transpose(dealt[:, block(jb)], spread[jb][:, t, :, :].rearrange("j u q -> j (u q)"), ident[:])
            nc.scalar.activation(weight[0][:, t, :], dealt[:], ACT.Copy, scale=gain_sb[:, 0, t : t + 1])
            if t < WEIGHTS_ON_SCALAR:
                nc.scalar.activation(weight[1][:, t, :], dealt[:], ACT.Copy, scale=gain_sb[:, 1, t : t + 1])
            else:
                nc.vector.tensor_scalar(weight[1][:, t, :], dealt[:], gain_sb[:, 1, t : t + 1], None, ALU.mult)

        def deal(rows, engine_copy, grouped):
            engine_copy(
                grouped[:].rearrange("p (t m i) -> p m i t", t=PACK, i=PACK),
                rows[:].rearrange("p i (m t) -> p m i t", t=PACK),
            )
            return grouped

        def deal_pair(rows, u, engine_copy, grouped):
            engine_copy(
                grouped[:].rearrange("p (e m i) -> p m i e", e=2, i=PACK),
                rows[:].rearrange("p i (m u e) -> p u m i e", u=2, e=2)[:, u],
            )
            return grouped

        def next_grouped(columns):
            return staged("grouped", [P, columns * PACK], BF16, GROUPED_RING)

        def quantize(codes, scales, grouped):
            nc.vector.quantize_mx(out=codes.bitcast(FP8X4), scales=scales, in_=grouped[:])

        def quantized(name, grouped):
            codes = held(name + "_codes", [P, PASS], I32)
            scales = held(name + "_scales", [P, PASS], U8)
            quantize(codes[:], scales[:], grouped)
            return codes, scales

        def raw_product(b, jb, raw_t, n):
            acc = bank(n)
            for a in range(2):
                nc.tensor.matmul_mx(
                    out=acc[:], lhsT=v2_codes[a][:, block(jb)].bitcast(FP8X4), lhsT_scale=v2_scales[a][:, block(jb)],
                    rhs=w2_sb[b][:, a, :].bitcast(FP4X4), rhs_scale=w2_plane[b][:, a, :],
                    start=(a == 0), stop=(a == 1),
                )
            nc.scalar.copy(raw_t, acc[:].rearrange("j (p t) -> j t p", t=PACK))
            return raw_t

        def bounded_product(w3_q, h, u, neg_t, n):
            acc = bank(n)
            chans = slice(u * 2 * P, (u + 1) * 2 * P)
            for a in range(2):
                for e in range(2):
                    entries = block(2 * h + e)
                    nc.tensor.matmul_mx(
                        out=acc[:, e * 2 * P : (e + 1) * 2 * P],
                        lhsT=v2_codes[a][:, entries].bitcast(FP8X4), lhsT_scale=v2_scales[a][:, entries],
                        rhs=w3_q[a][0][:, chans].bitcast(FP8X4), rhs_scale=w3_q[a][1][:, chans],
                        start=(a == 0 and e == 0), stop=(a == 1 and e == 1),
                    )
            nc.scalar.activation(neg_t, acc[:], ACT.Tanh, bias=zero[:], scale=-1.0)
            return neg_t

        def place(b, h, u, raw_ts, neg_t, n, square):
            diff = bank(n)
            for v in range(2):
                for e in range(2):
                    dst = diff[:, block(2 * v + e)]
                    nc.tensor.matmul(dst, neg_t[:, block(2 * e + v)], ident[:], start=True, stop=False, is_transpose=True)
                    nc.tensor.matmul(
                        dst, raw_ts[2 * h + e][:, 2 * u + v, :], ident[:], start=False, stop=True, is_transpose=True
                    )
            nc.scalar.activation(square, diff[:], ACT.Square, bias=zero[:])
            offsets = pos_sb[:, h * PIECE // LIST_COLS : (h + 1) * PIECE // LIST_COLS]
            for v in range(2):
                t = 2 * u + v
                nc.vector.tensor_tensor(
                    pages[b][t][:].indirect(offsets),
                    square[:, v * PIECE : (v + 1) * PIECE], weight[b][:, t, h * PIECE : (h + 1) * PIECE], ALU.mult,
                )

        def next_raw():
            return staged("raw_t", [P, PACK, P], F32, RING)[:]

        def next_scalar_out():
            return staged("scalar_out", [P, BANK], F32, RING)[:]

        def next_square():
            return staged("square", [P, BANK], F32, SQUARE_RING)[:]

        raw_banks = (0, 5, 6, 7)
        raw_tiles = [next_raw(), tenant("after_first_half", [P, PACK, P], F32)[:], next_raw(), next_raw()]
        raw = [raw_product(0, jb, raw_tiles[jb], raw_banks[jb]) for jb in range(PL // P)]
        w3_q0 = [quantized("w3_00", deal(w3_rows0[0], nc.vector.tensor_copy, next_grouped(PASS)))]
        w3_q0.append((held("w3_01_codes", [P, PASS], I32), held("w3_01_scales", [P, PASS], U8)))
        halves = [
            deal_pair(w3_rows0[1], 0, nc.vector.tensor_copy, next_grouped(2 * P)),
            deal_pair(w3_rows0[1], 1, nc.scalar.copy, tenant("after_w3_01", [P, 2 * P * PACK], BF16)),
        ]
        for u in range(2):
            chans = slice(u * 2 * P, (u + 1) * 2 * P)
            quantize(w3_q0[1][0][:, chans], w3_q0[1][1][:, chans], halves[u])
        neg = [bounded_product(w3_q0, 0, u, next_scalar_out(), raw_banks[u]) for u in range(2)]
        v_scales = tenant("after_w3_01", [P, S], U8)
        nc.vector.tensor_copy(v_scales[:], tab_plane[:, 0, :].indirect(offs_sb[:]))
        place(0, 0, 0, raw, neg[0], 1, next_square())
        place(0, 0, 1, raw, neg[1], 2, next_square())
        neg = [bounded_product(w3_q0, 1, 0, neg[1], raw_banks[2]), bounded_product(w3_q0, 1, 1, neg[0], 1)]
        place(0, 1, 0, raw, neg[0], 3, next_square())
        w3_q1 = [
            quantized("w3_10", deal(w3_rows1[0], nc.scalar.copy, tenant("after_first_half", [P, PASS * PACK], BF16))),
            quantized("w3_11", deal(w3_rows1[1], nc.scalar.copy, tenant("after_w3_11", [P, PASS * PACK], BF16))),
        ]
        place(0, 1, 1, raw, neg[1], 4, w3_rows1[1][:, 0, :])

        first_raw = tenant("after_third_half", [P, 2, PACK, P], F32)
        spent_rows = w3_rows1[1][:].rearrange("j i (t p) -> j i t p", t=PACK)
        raw_tiles = [first_raw[:, 0], first_raw[:, 1], spent_rows[:, 1], spent_rows[:, 2]]
        raw = [raw_product(1, jb, raw_tiles[jb], raw_banks[jb]) for jb in range(PL // P)]
        neg = [bounded_product(w3_q1, 0, u, next_scalar_out(), raw_banks[2 + u]) for u in range(2)]
        v_codes = tenant("after_w3_11", [P, S], I32)
        nc.vector.tensor_copy(v_codes[:].bitcast(U32), tab_sb[:].bitcast(U32).indirect(offs_sb[:]))
        place(1, 0, 0, raw, neg[0], 1, next_square())
        w1_q = [quantized("w1_0", deal(w1_rows[0], nc.scalar.copy, tenant("after_third_half", [P, PASS * PACK], BF16)))]
        place(1, 0, 1, raw, neg[1], 2, w1_rows[0][:, 0, :])
        neg = [bounded_product(w3_q1, 1, 0, neg[1], raw_banks[0]), bounded_product(w3_q1, 1, 1, neg[0], 1)]
        place(1, 1, 0, raw, neg[0], 3, next_square())
        place(1, 1, 1, raw, neg[1], 4, next_square())

        def gloss_product(b, t, cols, acc):
            nc.tensor.matmul_mx(
                out=acc, lhsT=w1_q[b][0][:, block(t)].bitcast(FP8X4), lhsT_scale=w1_q[b][1][:, block(t)],
                rhs=v_codes[:, cols].bitcast(FP8X4), rhs_scale=v_scales[:, cols], start=True, stop=True,
            )

        def combine_without_vector():
            gloss_banks = (3, 4, 1, 2)
            sum_banks = (5, 6)
            gloss, lift = [], []
            for t in range(PACK):
                acc = bank(gloss_banks[t])[:, :CHUNK]
                gloss_product(0, t, slice(0, CHUNK), acc)
                gloss.append(staged("raw_t", [P, CHUNK], F32, RING)[:])
                nc.scalar.copy(gloss[t], acc)
                lift.append(staged("scalar_out", [P, CHUNK], F32, RING)[:])
                nc.scalar.activation(lift[t], acc, ACT.Relu, bias=rest_sb[:, 0, t : t + 1], scale=-1.0)
            grouped = next_grouped(CHUNK)
            back = bank(gloss_banks[0])
            for jb in range(CHUNK // P):
                total = bank(sum_banks[jb])
                for t in range(PACK):
                    for k, term in enumerate((gloss[t], pages[0][t], lift[t])):
                        nc.tensor.matmul(
                            total[:, block(t)], term[:, block(jb)], ident[:],
                            start=(k == 0), stop=(k == 2), is_transpose=True,
                        )
                z_t = tenant("z_t%d" % jb, [P, 2, P, 2], BF16)
                nc.scalar.copy(z_t[:], total[:].rearrange("j (u v p) -> j u p v", u=2, v=2))
                pairs = z_t[:].rearrange("j u p v -> j (u p v)").bitcast(F32)
                for u in range(2):
                    nc.tensor.transpose(back[:, block(2 * jb + u)], pairs[:, block(u)], ident[:])
            words = grouped[:].bitcast(F32).rearrange("p (e j u) -> p e j u", e=2, u=2)
            nc.scalar.copy(words, back[:].rearrange("p (e u j) -> p e j u", e=2, u=2))
            return grouped

        def combine(b, c0, z, banks, weave, grouped):
            width = z.shape[2]
            cols = slice(c0, c0 + width)
            for t in range(PACK):
                acc = bank(banks[t])
                gloss_product(b, t, cols, acc[:, :width])
                nc.vector.scalar_tensor_tensor(
                    z[:, t, :], acc[:, :width], rest_sb[:, b, t : t + 1], pages[b][t][:, cols], ALU.max, ALU.add
                )
            weave(
                grouped[:].rearrange("p (c n t) -> p c t n", n=4, t=PACK),
                z[:].rearrange("p t (c n) -> p c t n", n=4),
            )
            return grouped

        z_first = combine_without_vector()
        w1_last = deal(w1_rows[1], nc.scalar.copy, tenant("after_third_half", [P, PASS * PACK], BF16))
        w1_q.append((tenant("z_t1", [P, PASS], I32), held("w1_1_scales", [P, PASS], U8)))
        quantize(w1_q[1][0][:], w1_q[1][1][:], w1_last)

        z_codes = [held("z_codes%d" % b, [P, S], I32) for b in range(2)]
        z_scales = [held("z_scales%d" % b, [P, S], U8) for b in range(2)]
        bank_sets = ((1, 2, 5, 3), (7, 0, 4, 6))
        z_second = combine(0, CHUNK, held("z_second", [P, PACK, CHUNK], BF16), bank_sets[1], nc.scalar.copy, next_grouped(CHUNK))
        z_third = combine(0, BANK, held("z_third", [P, PACK, BANK], BF16), bank_sets[0], nc.scalar.copy, next_grouped(BANK))
        for cols, grouped in ((slice(0, CHUNK), z_first), (slice(CHUNK, BANK), z_second), (slice(BANK, S), z_third)):
            quantize(z_codes[0][:, cols], z_scales[0][:, cols], grouped)

        chunks = S // CHUNK

        def finish(index, grouped):
            cols = slice(index * CHUNK, (index + 1) * CHUNK)
            quantize(z_codes[1][:, cols], z_scales[1][:, cols], grouped)
            acc = bank(bank_sets[(index + 1) % 2][index // 2])
            for b in range(2):
                for nt in range(N // P):
                    nc.tensor.matmul_mx(
                        out=acc[:, nt * CHUNK : (nt + 1) * CHUNK],
                        lhsT=w4_sb[:, b, block(nt)].bitcast(FP8X4), lhsT_scale=w4_plane[:, b, block(nt)],
                        rhs=z_codes[b][:, cols].bitcast(FP8X4), rhs_scale=z_scales[b][:, cols],
                        start=(b == 0 and nt == 0), stop=(b == 1 and nt == N // P - 1),
                    )
            features = staged("raw_t", [P, N // P, CHUNK], F32, RING)
            nc.scalar.activation(features[:].rearrange("p n j -> p (n j)"), acc[:], ACT.Sin, bias=zero[:])
            nc.sync.dma_start(out[:, cols].rearrange("(n p) j -> p n j", p=P), features[:])

        woven = []
        for index in range(chunks):
            weave = nc.vector.tensor_copy if index == chunks - 1 else nc.scalar.copy
            z = staged("square", [P, PACK, CHUNK], BF16, SQUARE_RING)
            grouped = staged("chunk_grouped", [P, CHUNK * PACK], BF16, chunks)
            woven.append(combine(1, index * CHUNK, z, bank_sets[(index + 1) % 2], weave, grouped))
            if index >= 2:
                finish(index - 2, woven[index - 2])
        for index in range(chunks - 2, chunks):
            finish(index, woven[index])
